import numpy as np, ml_dtypes
CORES = [3,7,11,15,131,135,139,143]
N = 8
BF = ml_dtypes.bfloat16
def gentries(a):
    return np.ascontiguousarray(a.reshape(8, 16, -1).transpose(0, 2, 1)).reshape(8, -1)
def gtable(e):
    e = np.asarray(e); return np.ascontiguousarray(e.reshape(8, -1, 16).transpose(0, 2, 1)).reshape(128, -1).astype(np.int32)
W, LN, M, RO, C = 2048, 256, 14, 5, 8
PM = [1, 4]
TOP = M - RO
def mates():
    return np.arange(N)[:, None] ^ np.array(PM)[np.arange(LN) // (LN // len(PM))][None, :]
def hashed(l, s):
    s = s[..., None, :]
    return ((l * s >> 5) + l + 37 * np.arange(M)[:, None] + s) & (W - 1)
def noisy(rng, base, share):
    e = rng.integers(-1, 2, (N, 8, 16, W)) * ((rng.random((N, 8, 1, W)) < share) & (rng.random((N, 8, 16, W)) < rng.random((N, 8, 1, W))))
    return np.clip(base + e, 0, 15)
def parts(rng, lo):
    x = noisy(rng, rng.integers(0, 16, (1, 8, 16, W)), 0.015625)
    n = np.maximum(rng.integers(lo, TOP + 1, (1, 8, LN)) - rng.integers(0, 4, (N, 8, LN)) * (rng.random((N, 8, LN)) < 0.12), 0)
    cut = np.where(rng.random((N, 8, LN)) < 0.12, n - rng.integers(1, 6, (N, 8, LN)), M)
    l = np.where(np.arange(M)[:, None] >= cut[:, :, None, :], rng.integers(0, W, (N, 8, M, LN)), rng.integers(0, W, (1, 8, M, LN)))
    s = np.repeat(rng.integers(0, 4096, (1, 8, RO, LN)), N, 0); w = np.repeat(rng.integers(0, 4096, (1, 8, 16)), N, 0)
    q = rng.random((1, 8, LN)); k = np.where(q < 0.6, 1, np.where(q < 0.9, rng.integers(1, 9, (1, 8, LN)), rng.integers(1, 9, (N, 8, LN))))
    few = np.array([0, 0, 1, 2, 4, 8, 16, 40]); th = np.where(rng.random((1, 8, LN)) < 0.9, rng.choice(few, (1, 8, LN)), rng.choice(few, (N, 8, LN)))
    return x, l, s, n, k, th, w
def lists(a):
    return np.stack([gtable(v.reshape(8, -1)) for v in a])
def pack(x, l, s, n, k, th, w):
    return {"xt": np.ascontiguousarray(x.reshape(N, 128, W)).astype(np.float32).astype(BF), "tr": lists(l), "sd": lists(s), "n0": lists(n), "k0": lists(k), "th": lists(th),
            "wt": np.ascontiguousarray(w.reshape(N, 128, 1)).astype(np.int32)}
def setup_inputs(rng):
    return pack(*parts(rng, max(TOP - 4, 1)))
def setup_inputs_spread(rng):
    x, l, s, n, k, th, w = parts(rng, 0)
    x = noisy(rng, np.floor(np.exp2(4 * rng.random((1, 8, 1, W))) * rng.random((1, 8, 16, W))).astype(np.int64), 0.03)
    l = l * l * l // (W * W); s = s * s // 4096; w = w * w // 4096
    th = np.repeat(np.clip(np.exp2(8.01 * rng.random((1, 8, LN))).astype(np.int64) - 1, 0, 255), N, 0)
    return pack(x, l, s, n, k, th, w)
def setup_inputs_ends(rng):
    par = np.array([bin(r).count("1") & 1 for r in range(N)])
    def two(p, *sh):
        return np.repeat((rng.random((1,) + sh) < p).astype(np.int64), N, 0)
    x = 15 * two(0.5, 8, 16, W); x = np.where(rng.random((N, 8, 1, W)) < 0.01, 15 - x, x)
    l = (W - 1) * two(0.5, 8, M, LN); l = np.where(rng.random(l.shape) < 0.01, W - 1 - l, l)
    s = 4095 * two(0.5, 8, RO, LN); w = 4095 * two(0.5, 8, 16)
    n = TOP * two(0.8, 8, LN); n = np.where(rng.random(n.shape) < 0.04, TOP - n, n)
    k = 1 + 7 * two(0.3, 8, LN); k = np.where(rng.random(k.shape) < 0.05, 9 - k, k)
    th = 255 * two(0.5, 8, LN); th = np.where(rng.random(th.shape) < 0.05, 255 - th, th)
    big = np.array([5, LN - 2, LN - 1])
    x[:, 7] = 15; w[:, 7] = 4095; n[:, 7] = TOP; k[:, 7] = 1 + 7 * par[:, None]; l[:, 7] = l[0, 7].copy()
    k7 = k[:, 7]; k7[:, big] = 1; s7 = s[:, 7]; s7[:, :, big] = 0
    k7[:, 9] = 1; l[:, 7, :, 9] = W - 1; s7[:, :, 9] = 0; s7[:, RO - 1, 9] = 4095; th[:, 7, 9] = 0
    z = (((W - 1) * 4095 >> 5) + W - 1 + 4095) & (W - 1); x7 = x[:, 7]; x7[par == 1, :, z] = 0
    x[:, 6] = 15 * par[:, None, None]; n[:, 6, LN - 1] = TOP
    x[:, 5] = x[0, 5].copy(); l[:, 5] = l[0, 5].copy()
    for r in range(N):
        y = x[r, 5]; y[15, 0] = 0; y[15, 37] = 0; y[3, 0] = 0; y[3, 74] = 0
        if par[r]:
            y[:, 0] = 15 - y[:, 0]; y[15, 37] = 15; y[3, 74] = 15
    for i in (4, LN - 1):
        n[:, 5, i] = TOP; k[:, 5, i] = 1; th[:, 5, i] = 255; s[:, 5, 0, i] = 0; l[:, 5, 0, i] = 0; l[:, 5, 1, i] = 0; l[:, 5, 2, i] = 0 if i == 4 else W - 1
    def alone(g, cols):
        own = cols // C; kg = k[:, g]; kg[:, own] = 1 + 7 * par[:, None]; i = int(np.setdiff1d(np.arange(LN), own)[-1])
        n[:, g, i] = TOP; k[:, g, i] = 1; l[:, g, :, i] = 0; s[:, g, :, i] = 0
        return i
    e0 = 37 * np.arange(M); e1 = (e0 - 1) & (W - 1); i = alone(4, np.concatenate([e0, e1])); y = x[:, 4]
    y[:, :, e0] = y[:1, :, e0]; y[:, :, e1] = y[:1, :, e1]; y[:, 15, e1] = 15 * par[:, None]
    w[:, 4] = 0; s[:, 4, RO - 1, i] = 4095; th[:, 4, i] = 120
    z = np.arange(65520, 0, -1); v = 15 * (M - 1) * z; ws = int(z[((v & 4095) == 4095) & ((v >> 12 & 1) == 1)][0])
    u = (15 * ws * np.arange(M)) & 4095; e0 = (np.where(np.arange(M) < TOP, 0, (u * u >> 5) + 37 * u) + 37 * np.arange(M)) & (W - 1)
    alone(3, e0); y = x[:, 3]; y[:, :, e0] = 15; w[:, 3] = np.clip(ws - 4095 * np.arange(16), 0, 4095)
    return pack(x, l, s, n, k, th, w)
def setup_inputs_corners(rng):
    x, l, s, n, k, th, w = parts(rng, 1)
    jj = np.arange(M)[:, None]; own = rng.integers(0, W, (N, 8, M, LN))
    kk = np.array([1, 1, 1, 2, 3, 4, 7, 8])
    n[:, 0] = 0; k[:, 0] = np.where(rng.random((1, LN)) < 0.7, rng.choice(kk, (1, LN)), rng.choice(kk, (N, LN)))
    x[:, 1] = x[0, 1].copy(); l[:, 1] = l[0, 1].copy(); n[:, 1] = TOP; k[:, 1] = 1; th[:, 1] = 0
    if W == 4096:
        l[:, 1, 0, ::4] = 4095; s[:, 1, :, ::4] = 4065
        l[:, 1, 0, 1::4] = 4093; s[:, 1, :, 1::4] = 4075
    x[:, 2] = x[0, 2].copy(); n[:, 2] = TOP; k[:, 2] = 8; th[:, 2] = 0; l[:, 2] = np.where(jj == TOP - 1, own[:, 2], l[0, 2].copy())
    x[:, 3] = x[0, 3].copy(); k[:, 3] = 6; th[:, 3] = 0; n[:, 3] = rng.integers(4, TOP + 1, (1, LN))
    cut = n[:, 3] - rng.integers(0, 5, (N, LN)); l[:, 3] = np.where(jj >= cut[:, None, :], own[:, 3], l[0, 3].copy())
    s[:, 4] = rng.integers(0, 4096, (N, RO, LN)); w[:, 4] = rng.integers(0, 4096, (N, 16)); k[:, 4] = rng.integers(1, 9, (N, LN)); th[:, 4] = rng.choice(np.array([0, 60, 255]), (N, LN))
    n[:, 5] = rng.choice(np.array([0, 1, TOP]), (N, LN)); n[:, 5, :LN // 2] = rng.choice(np.array([0, 1, TOP]), (1, LN // 2))
    n[:, 6] = n[0, 6].copy(); k[:, 6] = 1
    ix = hashed(l[:, 6], s[:, 6, 0]); v = np.take_along_axis(x[:, 6], ix.reshape(N, 1, -1), 2).reshape(N, 16, M, LN)
    p = np.add.reduce(np.where(jj < n[:, 6][:, None, None, :], v, 0), axis=2)
    d = np.add.reduce(np.abs(p - np.take_along_axis(p, mates()[:, None, :], 0)), axis=1)
    th[:, 6] = np.clip(d + rng.integers(-1, 2, d.shape), 0, 255)
    return pack(x, l, s, n, k, th, w)
def setup_inputs_crowd(rng):
    x, l, s, n, k, th, w = parts(rng, 1)
    par = np.array([bin(r).count("1") & 1 for r in range(N)]); jj = np.arange(M)[:, None]
    x = np.repeat(x[:1], N, 0); l = np.repeat(l[:1], N, 0); nb = rng.integers(1, TOP, (1, 8, LN))
    l[:, 2] = l[:, 2, :, :1].copy(); s[:, 2] = s[:, 2, :, :1].copy(); nb[:, 2] = nb[:, 2, :1].copy()
    l[:, 4, :, :LN - 1] = l[:, 4, :, :1].copy(); s[:, 4, :, :LN - 1] = s[:, 4, :, :1].copy()
    nb[:, 3] = rng.integers(3, min(TOP, 7), (1, LN))
    hit = hashed(l[0, 3], s[0, 3, 0])[:, :LN - 2][jj <= nb[0, 3, :LN - 2][None, :]]; left = np.setdiff1d(np.arange(W), hit)
    c0 = int(rng.choice(left)); c1 = int(rng.choice(left[((left - c0) % W > 128) & ((c0 - left) % W > 128)]))
    for i, c in ((LN - 1, c0), (LN - 2, c1)):
        l[:, 3, :, i] = (c - 37 * np.arange(M)) & (W - 1); s[:, 3, 0, i] = 1; s[:, 3, 1, i] = 0; nb[:, 3, i] = 3
    n = nb + par[:, None, None]; k = np.ones((N, 8, LN), np.int64); th = np.zeros((N, 8, LN), np.int64)
    for r in (0, PM[-1]):
        k[r, 7, LN - 1] = 2; th[r, 7, LN - 1] = 255
    ix = hashed(l[0], s[0, :, 0]); live = jj <= nb[0][:, None, :]
    used = np.zeros((8, W), bool); np.put_along_axis(used, np.where(live, ix, ix[:, :1]).reshape(8, -1), True, 1)
    e = rng.integers(-1, 2, x.shape) * ((rng.random((N, 8, 1, W)) < 0.04) & (rng.random(x.shape) < 0.2) & ~used[None, :, None, :])
    x = np.clip(x + e, 0, 15)
    z = hashed(l[0, 7], s[0, 7, 1])[:, LN - 1]; x7 = x[:, 7]; x7[:, :, z] = x7[:1, :, z]; x7[:, :, int(z[nb[0, 7, LN - 1]])] = 0
    y = np.where(par[:, None, None] == 1, rng.integers(5, 10, (N, 16, W)), rng.integers(0, 4, (N, 16, W)))
    x[:, 3] = np.where(used[3], x[:, 3], y)
    for c, g in ((c0, 87), (c1, 90)):
        x[:, 3, :, c] = x[0, 3, :, c].copy(); x[:, 3, :8, c] = par[:, None] * ((g + np.arange(8)) >> 3)
    ix = hashed(l[:, 3], s[:, 3, 1]); v = np.take_along_axis(x[:, 3], ix.reshape(N, 1, -1), 2).reshape(N, 16, M, LN)
    p = np.add.reduce(np.where(jj < nb[0, 3][None, :], v, 0), axis=2)
    d = np.add.reduce(np.abs(p - np.take_along_axis(p, mates()[:, None, :], 0)), axis=1)
    for r in (0, PM[-1]):
        th[r, 3] = np.clip(d[r] - 15 + rng.integers(-1, 2, LN), 0, 255)
        th[r, 3, LN - 1] = 245; th[r, 3, LN - 2] = 255
    return pack(x, l, s, n, k, th, w)
def setup_inputs_few(rng):
    x, l, s, n, k, th, w = parts(rng, 1)
    par = np.array([bin(r).count("1") & 1 for r in range(N)]); h = LN // 2
    x = np.repeat(x[:1], N, 0); l = np.repeat(l[:1], N, 0); n = np.repeat(n[:1], N, 0); k = np.repeat(k[:1], N, 0)
    n[:, 3:] = rng.integers(1, min(TOP, 15), (1, 5, LN)) + par[:, None, None]; k[:, 3:] = 8
    D = rng.integers(1, 17, (4, 1, 1)); e = (np.argsort(rng.random((4, 16, W)), axis=1) < D).astype(np.int64)
    x[:, 3:7] = np.minimum(x[:, 3:7], 14) + e[None] * par[:, None, None, None]
    l[:, 3:7, :, h:] = rng.integers(0, W // 8, (1, 4, M, LN - h)); s[:, 3:7, :, h:] = rng.integers(0, 32, (1, 4, RO, LN - h))
    m = rng.integers(5, 7, (4, LN - h)); n[:, 3:7, h:] = m
    z = np.stack([rng.permutation(LN - h) % 10 for g in range(4)])
    th[:, 3:7, h:] = np.where(par[:, None, None] == z // 5, m * D[:, :, 0] - z % 5, 0)
    ty = rng.permutation(N) % 4; o = rng.permutation(h)
    for r in range(N):
        for j in range(int(ty[r])):
            n[r, 7 - j, o[r]] = 0; k[r, 7 - j, o[r]] = (1, 6, 5)[j]
    return pack(x, l, s, n, k, th, w)
def check_inputs(d):
    bad = []
    for a, lo, hi in (("xt", 0, 15), ("tr", 0, W - 1), ("sd", 0, 4095), ("n0", 0, TOP), ("k0", 1, 8), ("th", 0, 255), ("wt", 0, 4095)):
        v = np.asarray(d[a]).astype(np.float64)
        if not (np.all(v >= lo) and np.all(v <= hi)): bad.append("range of " + a)
        elif np.any(v != np.floor(v)): bad.append("whole numbers in " + a)
    return bad
def reference(xt, tr, sd, n0, k0, th, wt):
    X = xt.astype(np.float32).astype(np.int32).reshape(N, 8, 16, W); wv = wt.astype(np.int64).reshape(N, 8, 16, 1)
    L = np.stack([gentries(a) for a in tr]).astype(np.int64).reshape(N, 8, M, LN)
    S = np.stack([gentries(a) for a in sd]).astype(np.int64).reshape(N, 8, RO, LN)
    n = np.stack([gentries(a) for a in n0]).astype(np.int64); k = np.stack([gentries(a) for a in k0]).astype(np.int64)
    t0 = np.stack([gentries(a) for a in th]).astype(np.int64)
    v1 = np.zeros((N, 8, LN), np.int64); v2 = np.zeros((N, 8, LN), np.int64); A = np.zeros((N, 1, 1), np.int64)
    mate = mates(); jj = np.arange(M)[:, None]; ii = np.arange(LN)
    def other(a):
        return np.take_along_axis(a, mate.reshape((N,) + (1,) * (a.ndim - 2) + (LN,)), 0)
    for rnd in range(RO):
        ix = hashed(L, S[:, :, rnd])
        V = np.take_along_axis(X, ix.reshape(N, 8, 1, M * LN), 3).reshape(N, 8, 16, M, LN)
        R = np.concatenate([np.zeros((N, 8, 16, 1, LN), np.int32), np.add.accumulate(V, axis=3, dtype=np.int32)], axis=3)
        K = np.where(k >= 8, 8, np.where(k >= 4, 4, np.where(k >= 2, 2, 1)))
        m1 = n - (n & (K - 1)); m2 = np.maximum(m1 - K, 0)
        Pn, P1, P2 = [np.take_along_axis(R, m[:, :, None, None, :], 3)[:, :, :, 0] for m in (n, m1, m2)]
        lim = t0 + (A & 15)
        def agree(a, la, b, lb):
            return (la == lb) & (np.add.reduce(np.abs(a - b), axis=2) <= lim)
        Q1, q1, Q2, q2 = other(P1), other(m1), other(P2), other(m2)
        ok = agree(Pn, n, other(Pn), other(n)) & (k == other(k))
        a1 = agree(P1, m1, Q1, q1) | agree(P1, m1, Q2, q2)
        a2 = agree(P2, m2, Q1, q1) | agree(P2, m2, Q2, q2)
        u = np.add.reduce(wv * Pn, axis=2) & 4095; new = ((u * u >> 5) + 37 * u) & (W - 1)
        L = np.where((jj == n[:, :, None, :]) & ok[:, :, None, :], new[:, :, None, :], L)
        col = (C * ii + (u & (C - 1)))[:, :, None, :]
        np.put_along_axis(X, col, np.where(ok[:, :, None, :], Pn >> 4, np.take_along_axis(X, col, 3)).astype(np.int32), 3)
        c1 = v1 + a1; c2 = v2 + a2; full = ~ok & (k + 1 == 2 * K)
        b1 = full & (2 * c1 >= K); b2 = full & ~b1 & (2 * c2 >= K)
        n = np.where(ok, n + 1, np.where(b1, m1, np.where(b2, m2, n)))
        k = np.where(ok | b1 | b2, 1, k + 1)
        v1 = np.where(ok | full, 0, c1); v2 = np.where(ok | full, 0, c2)
        A = np.add.reduce((b1 | b2).astype(np.int64), axis=(1, 2), keepdims=True)
    st = np.stack([n, k, v1, v2], axis=2)
    return {"yt": lists(L).astype(np.float32), "yst": lists(st).astype(np.float32), "yx": np.ascontiguousarray(X.reshape(N, 128, W)).astype(np.float32).astype(BF)}

@@ -1,0 +1,504 @@
+import numpy as np
+from concourse.bass import DstId, RemoteDMATransfer
+from concourse.mybir import AluOpType, ActivationFunctionType
+
+RO, TOP, SLOTS, W = 5, 9, 14, 2048
+PM = (1, 4)
+F, B, I, U, H = "float32", "bfloat16", "int32", "uint16", "float16"
+
+
+def _sb(n, d):
+    return ("sbuf", [128] + (n if isinstance(n, list) else [n]), d)
+
+
+SCRATCH = {
+    "X": _sb(2 * W, B), "G": _sb(256 * 14, B), "R": _sb(256 * 14, B), "ZE": _sb(128 * 14, B),
+    "S1": _sb([RO, 2, 160], B), "L1": _sb([RO, 2, 160], B), "S2": _sb([RO, 2, 256], B), "L2": _sb([RO, 2, 256], B),
+    "tri": _sb(224, I), "sdi": _sb(80, I), "n0i": _sb(16, I), "k0i": _sb(16, I), "thi": _sb(16, I), "wti": _sb(1, I),
+    "TT": _sb(224, F), "S32": _sb(80, F), "SR": _sb(224, F), "DL": _sb(224, H), "DK": _sb(224, H), "EQ": _sb(224, F),
+    "IF": _sb(128, F), "NF": _sb(128, F), "IH": _sb(128, H), "NH": _sb(128, H), "C32": _sb(224, B),
+    "EA": _sb(224, F), "YI": _sb(224, I), "YB": _sb(224, I), "CI": _sb(224, U), "BE": _sb(224, F), "JC": _sb(224, B),
+    "IC": _sb(144, F), "SEL": _sb(144, B), "WM": _sb(144, H), "ID": _sb(128, B), "NI": _sb(128, B), "ON": _sb(128, B),
+    "pi": _sb(1, I), "pa": _sb(1, I), "pb": _sb(1, I), "pf": _sb(1, F), "gf": _sb(1, F), "pm": _sb(1, F),
+    "wa": _sb(1, I), "wb": _sb(1, I), "wf": _sb(1, F),
+    "REP": _sb(16, U), "IA": _sb(16, F), "IB": _sb(48, F), "IL": _sb(48, F), "BC": _sb(16, F), "OB": _sb(48, F),
+    "OF": _sb(48, F), "OU": _sb(48, U), "THR": _sb([2, 40], F), "LI": _sb([2, 40], F), "E": _sb([2, 48], F),
+    "LM": _sb([2, 40], F), "AN": _sb(256, B), "AR": _sb(1024, B), "VAL": _sb(256, B), "C192": _sb(256, B),
+    "ui": _sb(16, I), "uu": _sb(16, I), "u7": _sb(16, I), "w1": _sb(16, F), "w2": _sb(16, F), "pr": _sb(16, I), "nw": _sb(16, I),
+    "NEW": _sb(32, H), "c1": _sb(16, F), "CF": _sb(16, F), "bad": _sb(16, F), "sy": _sb(16, F), "SO": _sb(16, U),
+    "ok": _sb(16, B), "AG": _sb([2, 32], F), "av": _sb([2, 16], F), "cv": _sb([2, 16], F), "V": _sb([2, 16], F),
+    "PT": _sb([2, 4, 8], F), "RQ": _sb([2, 2, 8], F), "keep": _sb(16, B), "wn": _sb(16, F), "xn": _sb(16, F), "nor": _sb(16, F),
+    "t0": _sb(16, F), "t1": _sb(16, F), "K": _sb(16, F), "CC": _sb(16, F), "BB": _sb(16, F), "zz": _sb(16, F),
+    "MR": _sb([2, 16], F), "ek": _sb(16, F), "nf": _sb(16, F), "uh": _sb(16, F), "HK": _sb(16, F), "gk": _sb(16, F),
+    "K2": _sb(16, F), "kv": _sb(16, F), "b2": _sb(16, F), "b4": _sb(16, F), "b8": _sb(16, F),
+    "aj": _sb(16, F), "nx": _sb(1, F), "r1": _sb(1, F), "r2": _sb(1, F), "r3": _sb(1, F), "a15": _sb(1, F),
+    "YS": _sb(64, F), "YT": _sb(224, F),
+}
+for _i in range(8):
+    SCRATCH["P%d" % _i] = ("psum", [128, 512], F)
+
+SEMAPHORES = (["cv_", "cs_", "ct_", "cg_", "loc"] + ["d%d" % i for i in range(10)]
+              + ["a%d_%d" % (t, h) for t in range(RO) for h in range(2)]
+              + ["b%d" % t for t in range(RO)] + ["c%d" % t for t in range(RO)])
+
+NV = [3, 2, 3, 3, 3]
+NE = [0, 2, 2, 2, 2]
+ND = [3, 4, 4, 4, 4]
+BIG = 1.5 * 2.0 ** 23
+AL = AluOpType
+AF = ActivationFunctionType
+S_ = np.s_
+
+
+def rank_program(g, core, T, topo):
+    rank = T.rank_of(core)
+    if rank is None:
+        return
+    Q = {"v": g.vector, "s": g.scalar, "t": g.tensor, "g": g, "y": g.sync}
+    OWN = {"v": "cv_", "s": "cs_", "t": "ct_", "g": "cg_"}
+    cnt = {}
+    seen = {q: {} for q in Q}
+    prod = [None]
+    ids, lw, lr, bank = {}, {}, {}, {}
+    for nm, (where, shp, dty) in SCRATCH.items():
+        n = int(np.prod(shp[1:]))
+        ids[nm] = np.arange(n).reshape([1] + shp[1:])
+        lw[nm] = np.zeros(n, np.int64)
+        lr[nm] = {}
+        if where == "psum":
+            bank[nm] = {}
+
+    def A(nm, idx=None):
+        return (nm, S_[:] if idx is None else idx)
+
+    def X(win, off):
+        return (win[0], win[1], off)
+
+    def ap(a):
+        if isinstance(a, tuple):
+            v = T[a[0]][a[1]]
+            return v.indirect(ap(a[2])) if len(a) == 3 else v
+        return a
+
+    def parts(a):
+        if not isinstance(a, tuple):
+            return []
+        return [a[:2], a[2]] if len(a) == 3 else [a]
+
+    def wait(q, sem, val):
+        if seen[q].get(sem, 0) < val:
+            seen[q][sem] = val
+            Q[q].wait_ge(T.sem[sem], val)
+
+    def mark(a, sem, val):
+        prod.append((sem, val))
+        cnt[sem] = val
+        lw[a[0]][ids[a[0]][a[1]].ravel()] = len(prod) - 1
+
+    def order(q, rd, wr, sem, val):
+        need = {}
+        own = OWN.get(q)
+
+        def add(p, same):
+            s, v = prod[p]
+            if (same or s != own) and need.get(s, 0) < v:
+                need[s] = v
+        prod.append((sem, val))
+        me = len(prod) - 1
+        for a in rd:
+            if a[0] in lw:
+                for p in np.unique(lw[a[0]][ids[a[0]][a[1]].ravel()]):
+                    if p:
+                        add(int(p), True)
+        for a in wr:
+            if a[0] in lw:
+                e = ids[a[0]][a[1]].ravel()
+                for arr in [lw[a[0]]] + list(lr[a[0]].values()):
+                    for p in np.unique(arr[e]):
+                        if p:
+                            add(int(p), False)
+        for a in rd + wr:
+            if a[0] in bank:
+                for s, p in bank[a[0]].items():
+                    add(p, False)
+        for s, v in need.items():
+            wait(q, s, v)
+        for a in rd:
+            if a[0] in lw:
+                if sem not in lr[a[0]]:
+                    lr[a[0]][sem] = np.zeros(len(lw[a[0]]), np.int64)
+                lr[a[0]][sem][ids[a[0]][a[1]].ravel()] = me
+        for a in wr:
+            if a[0] in lw:
+                lw[a[0]][ids[a[0]][a[1]].ravel()] = me
+        for a in rd + wr:
+            if a[0] in bank:
+                bank[a[0]][sem] = me
+
+    def emit(q, fn, outs, ins):
+        sem = OWN[q]
+        cnt[sem] = cnt.get(sem, 0) + 1
+        rd, wr = [], []
+        for a in ins:
+            rd += parts(a)
+        for a in outs:
+            p = parts(a)
+            wr += p[:1]
+            rd += p[1:]
+        order(q, rd, wr, sem, cnt[sem])
+        fn().then_inc(T.sem[sem], 1)
+
+    def tt(o, a, b, op):
+        emit("v", lambda: g.vector.tensor_tensor(ap(o), ap(a), ap(b), op), [o], [a, b])
+
+    def ts(o, a, s1, op0, s2=None, op1=None):
+        if op1 is None:
+            emit("v", lambda: g.vector.tensor_scalar(ap(o), ap(a), ap(s1), None, op0), [o], [a, s1])
+        else:
+            emit("v", lambda: g.vector.tensor_scalar(ap(o), ap(a), ap(s1), ap(s2), op0, op1), [o], [a, s1, s2])
+
+    def cp(o, a):
+        emit("v", lambda: g.vector.tensor_copy(ap(o), ap(a)), [o], [a])
+
+    def fill(o, c):
+        emit("v", lambda: g.vector.memset(ap(o), c), [o], [])
+
+    def act(o, a, fn=AF.Identity, bias=0.0, scale=1.0, acc=None):
+        if acc is not None:
+            emit("s", lambda: g.scalar.activation(ap(o), ap(a), fn, bias, scale, accum_out=ap(acc)), [o, acc], [a])
+        else:
+            emit("s", lambda: g.scalar.activation(ap(o), ap(a), fn, ap(bias), scale), [o], [a, bias])
+
+    def mm(o, l, r, st, sp):
+        emit("t", lambda: g.tensor.matmul(ap(o), ap(l), ap(r), st, sp), [o], [l, r])
+
+    def iota(o, pat, base, cm):
+        if SCRATCH[o[0]][2] == I:
+            emit("g", lambda: g.iota(ap(o), pat, base, cm), [o], [])
+        else:
+            emit("g", lambda: g.iota(ap(o), pat, base, cm, allow_small_or_imprecise_dtypes=True), [o], [])
+
+    nd = [0]
+
+    def dma(q, o, a):
+        sem = "d%d" % nd[0]
+        nd[0] += 1
+        cnt[sem] = 16
+        order(q, [a], [o], sem, 16)
+        Q[q].dma_start(ap(o), ap(a)).then_inc(T.sem[sem], 16)
+
+    mate = [T.cores[rank ^ d] for d in PM]
+    eng = [list(topo.engines(core, m)) for m in mate]
+    far = 0 if len(eng[0]) < len(eng[1]) else 1
+    near = 1 - far
+    eng[near] = [e for e in eng[near] if e not in eng[far]]
+    msk = [sum(1 << e for e in es) for es in eng]
+    total = len(eng[0]) + len(eng[1])
+    dst = []
+    for m in mate:
+        rid, pid = topo.addr(m, core)
+        dst.append(DstId(rid=rid, pnc=pid))
+    for t in range(RO):
+        for h in range(2):
+            mark(A("L1", S_[:, t, h, 32:160]), "a%d_%d" % (t, h), len(eng[h]))
+        mark(A("L1", S_[:, t, :, 0:32]), "c%d" % t, total)
+        mark(A("L2", S_[:, t]), "b%d" % t, total)
+
+    def send(src, land, sem, t, halves, a, b):
+        cnt["loc"] = cnt.get("loc", 0) + sum(len(eng[h]) for h in halves)
+        order("g", [A(src, S_[:, t, h, a:b]) for h in halves], [], "loc", cnt["loc"])
+        g.remote_dma_fused([RemoteDMATransfer(dst_ids=[dst[h]], dma_engine_mask=msk[h], remote_sem=T.sem[sem],
+                                              src=T[src][:, t, h, a:b], dst=T[land][:, t, h, a:b]) for h in halves],
+                           local_sem=T.sem["loc"])
+
+    def st(t, a, b=None):
+        return A("S1", S_[:, t, :, 8 * a:8 * (a + 1 if b is None else b)])
+
+    def lst(t, a, b=None):
+        return A("L1", S_[:, t, :, 8 * a:8 * (a + 1 if b is None else b)])
+
+    def c(nm, a, b):
+        return A(nm, S_[:, a:b])
+
+    def hs(nm, a, b):
+        return A(nm, S_[:, :, a:b])
+
+    XT = c("X", 0, W)
+
+    dma("y", A("tri"), A("tr"))
+    dma("s", A("sdi"), A("sd"))
+    dma("y", XT, A("xt"))
+    dma("s", A("k0i"), A("k0"))
+    dma("s", A("n0i"), A("n0"))
+    dma("s", A("wti"), A("wt"))
+    dma("s", A("thi"), A("th"))
+    iota(A("pi"), [[0, 1]], 0, 1)
+    iota(A("IC"), [[1, 144]], 0, 0)
+    iota(A("BE"), [[1184, SLOTS], [0, 16]], -1024, 0)
+    iota(A("IB"), [[0, 6], [16, 8]], 0, 0)
+    iota(A("IA"), [[16, 16]], 0, 0)
+    iota(A("G", S_[:, 0:256 * (TOP + 1):TOP + 1]), [[0, 256]], -256, 0)
+    iota(A("JC"), [[1, SLOTS], [0, 16]], 0, 0)
+    fill(A("ZE"), 0.0)
+    ts(A("pa"), A("pi"), 15, AL.bitwise_and)
+    ts(A("pb"), A("pi"), 112, AL.bitwise_and)
+    cp(A("pf"), A("pi"))
+    cp(A("pm"), A("pa"))
+    ts(A("gf"), A("pb"), 15.0, AL.add)
+    ts(A("REP"), c("ZE", 0, 16), A("pm"), AL.add)
+    ts(A("ID"), c("IC", 0, 128), A("pf"), AL.is_equal)
+    act(A("NI"), A("ID"), AF.Identity, 0.0, -1.0)
+    act(A("IF"), A("ID"), AF.Copy)
+    act(A("NF"), A("ID"), AF.Identity, 0.0, -1.0)
+    ts(A("SEL"), A("IC"), A("gf"), AL.is_equal)
+    ts(A("IH"), c("IC", 0, 128), A("pf"), AL.is_equal)
+    ts(A("NH"), c("IC", 0, 128), A("pf"), AL.is_equal, -1.0, AL.mult)
+    fill(A("C32"), 32.0)
+    fill(A("C192"), -192.0)
+    fill(A("ON"), 1.0)
+    fill(A("V"), 0.0)
+    ts(A("IL"), A("IB"), A("pm"), AL.add)
+    ts(A("BC"), A("IA"), A("pm"), AL.add, 8.0 / W, AL.mult)
+
+    def rep_seed(t):
+        k = TOP + t
+        act(c("SR", 0, 16 * k), X(c("S32", 16 * t, 16 * t + 16), c("REP", 0, k)), AF.Copy)
+
+    def hash_tail(src, t):
+        n = 16 * (TOP + t)
+        tt(c("P7", 256, 256 + n), src, c("SR", 0, n), AL.mult)
+        tt(c("YI", 0, n), c("P7", 256, 256 + n), c("BE", 0, n), AL.add)
+        ts(c("YB", 0, n), c("YI", 0, n), 5, AL.logical_shift_right, W - 1, AL.bitwise_and)
+        cp(c("CI", 0, n), c("YB", 0, n))
+
+    def rounders(src):
+        ts(A("CC"), A(src), 1.0, AL.max, 2.0 ** 23 - 0.5, AL.mult)
+        ts(A("BB"), A(src), 1.0, AL.max, 2.0 ** 23, AL.mult)
+
+    def points_of(t):
+        tt(A("zz"), st(t, 1), A("CC"), AL.add)
+        tt(hs("MR", 0, 8), A("zz"), A("BB"), AL.subtract)
+        tt(hs("MR", 8, 16), hs("MR", 0, 8), A("K"), AL.subtract)
+        ts(st(t, 2, 4), A("MR"), 0.0, AL.max, 0.25, AL.add)
+        tt(A("OF"), st(t, 1, 4), A("OB"), AL.add)
+        cp(A("OU"), A("OF"))
+
+    ts(A("S32"), A("sdi"), 32.0, AL.add)
+    ts(A("TT"), A("tri"), 32.0, AL.add)
+    rep_seed(0)
+    act(A("OB"), A("IL"), AF.Identity, -0.25, float(TOP + 1))
+    hash_tail(c("TT", 0, 16 * TOP), 0)
+
+    def first_state():
+        ts(A("b2"), A("k0i"), 2.0, AL.is_ge, 1.0, AL.add)
+        ts(A("b4"), A("k0i"), 4.0, AL.is_ge, 4.0, AL.mult)
+        ts(A("b8"), A("k0i"), 8.0, AL.is_ge, 8.0, AL.mult)
+        tt(A("t0"), A("b2"), A("b4"), AL.max)
+        ts(st(0, 1), A("n0i"), 0.25, AL.add)
+        tt(A("K"), A("t0"), A("b8"), AL.max)
+        ts(st(0, 0), A("k0i"), 0.5, AL.mult)
+        rounders("K")
+        points_of(0)
+        ts(A("wa"), A("wti"), 2048.0, AL.add)
+        ts(hs("THR", 0, 8), A("thi"), 1.0, AL.add)
+        ts(A("wb"), A("wa"), 4095, AL.bitwise_and)
+        ts(A("wf"), A("wb"), -2048.0, AL.add)
+        ts(A("WM"), A("IC"), A("gf"), AL.is_equal, A("wf"), AL.mult)
+
+    def rows(o, mat, src):
+        for p in range(16):
+            mm(o, c(mat, 15 - p, 143 - p), src(p), p == 0, p == 15)
+
+    def gather(q, t, j, h):
+        L = TOP + t + 1
+        if h is None:
+            o, off = A("G", S_[:, 1 + j:256 * L:L]), c("CI", 16 * j, 16 * j + 16)
+        else:
+            o, off = A("G", S_[:, 128 * L * h + 1 + j:128 * L * (h + 1):L]), c("CI", 16 * j + 8 * h, 16 * j + 8 * h + 8)
+        if q == "v":
+            cp(o, X(XT, off))
+        else:
+            act(o, X(XT, off), AF.Copy)
+
+    for t in range(RO):
+        J = TOP + t
+        L = J + 1
+        n = 16 * L
+        last = t == RO - 1
+
+        def win(nm, h):
+            return c(nm, 128 * L * h, 128 * L * (h + 1))
+
+        def scan(h):
+            o, d0, d1 = win("R", h), win("G", h), c("ZE", 0, 128 * L)
+            emit("v", lambda: g.vector.tensor_tensor_scan(ap(o), ap(d0), ap(d1), 0.0, AL.add, AL.max), [o], [d0, d1])
+
+        def pn(nm, h):
+            return A(nm, S_[:, t, h, 32:160])
+
+        nv, ndf = NV[t], ND[t]
+        for j in range(nv, J - ndf):
+            gather("s", t, j, None)
+        for h in (far, near):
+            for j in range(J - ndf, J):
+                gather("s", t, j, h)
+        if t == 0:
+            first_state()
+        for j in range(NE[t], nv):
+            gather("v", t, j, None)
+        mm(c("P0", 256, 256 + n), A("NI"), c("JC", 0, n), True, False)
+        for j in range(L):
+            mm(c("P0", 256 + 16 * j, 272 + 16 * j), A("ID"), st(t, 1), False, j == L - 1)
+        mm(c("P6", 0, n), A("NF"), c("TT", 0, n), True, False)
+        mm(c("P6", 0, n), A("ID"), c("C32", 0, n), False, False)
+        if not last:
+            mm(c("P7", 0, n), A("IF"), c("TT", 0, n), True, False)
+        send("S1", "L1", "c%d" % t, t, [0, 1], 0, 32)
+        scan(far)
+        act(pn("S1", far), X(win("R", far), c("OU", 24 * far, 24 * far + 8)), AF.Copy)
+        send("S1", "L1", "a%d_%d" % (t, far), t, [far], 32, 160)
+        act(A("S2", S_[:, t, far, :]), X(win("R", far), c("OU", 24 * far + 8, 24 * far + 24)), AF.Copy)
+        scan(near)
+        cp(pn("S1", near), X(win("R", near), c("OU", 24 * near, 24 * near + 8)))
+        send("S1", "L1", "a%d_%d" % (t, near), t, [near], 32, 160)
+        act(A("S2", S_[:, t, near, :]), X(win("R", near), c("OU", 24 * near + 8, 24 * near + 24)), AF.Copy)
+        send("S2", "L2", "b%d" % t, t, [0, 1], 0, 256)
+        if not last:
+            iota(A("G", S_[:, 0:256 * (L + 1):L + 1]), [[0, 256]], -256, 0)
+
+        PN = A("S1", S_[:, t, :, 32:160])
+        rows(c("P3", 16, 32), "WM", lambda p: A("S1", S_[:, t, :, 32 + p:160:16]))
+        act(c("EA", 0, n), c("P0", 256, 256 + n), AF.Abs, -0.25)
+        if t:
+            m = n - 16
+            tt(c("DK", 0, m), c("DL", 0, m), c("P5", 0, m), AL.mult)
+            mm(c("P6", 0, m), A("NH"), c("DK", 0, m), False, False)
+            if not last:
+                mm(c("P7", 0, m), A("IH"), c("DK", 0, m), False, False)
+            tt(A("kv"), A("bad"), A("nf"), AL.mult)
+            tt(hs("V", 0, 8), hs("cv", 0, 8), A("kv"), AL.mult)
+            tt(hs("V", 8, 16), hs("cv", 8, 16), A("kv"), AL.mult)
+        DN = {far: c("P0", 0, 128), near: c("P5", 256, 384)}
+        for h in (far, near):
+            mm(DN[h], A("ID"), pn("S1", h), True, False)
+        for h in range(2):
+            mm(c("P%d" % (1 + h), 0, 256), A("ID"), A("S2", S_[:, t, h, :]), True, False)
+        ts(A("ek"), st(t, 0), 0.5, AL.add)
+        tt(A("nf"), A("ek"), A("K"), AL.not_equal)
+        act(c("EQ", 0, n), c("EA", 0, n), AF.Relu, 1.0, -1.0)
+        if not last:
+            rep_seed(t + 1)
+        act(A("uh"), A("nf"), AF.Identity, 0.5, 64.0)
+        act(A("gk"), A("nf"), AF.Identity, 2.0, -1.0)
+        if t:
+            act(A("aj"), c("P4", 64, 80), AF.Identity, 0.0, -1.0, A("nx"))
+            act(A("r1"), A("nx"), AF.Identity, -0.46875, 1.0 / 16)
+            act(A("r2"), A("r1"), AF.Identity, BIG)
+            act(A("r3"), A("r2"), AF.Identity, -BIG)
+            act(A("a15"), A("r3"), AF.Identity, A("nx"), -16.0)
+            act(A("LI"), A("THR"), AF.Identity, A("a15"))
+        else:
+            for k in range(1, 5):
+                act(hs("THR", 8 * k, 8 * k + 8), hs("THR", 0, 8), AF.Copy)
+        lim = "LI" if t else "THR"
+        act(A("VAL"), PN, AF.Identity, 191.53125, 1.0 / 16)
+        if not last:
+            act(A("OB"), A("IL"), AF.Identity, -0.25, float(L + 1))
+        cp(A("ui"), c("P3", 16, 32))
+        ts(A("uu"), A("ui"), 4095, AL.bitwise_and)
+        ts(A("u7"), A("ui"), 7, AL.bitwise_and)
+        ts(A("w1"), A("uu"), -2048.0, AL.add)
+        ts(A("w2"), A("uu"), 3232.0, AL.add)
+        tt(A("pr"), A("w1"), A("w2"), AL.mult)
+        ts(A("c1"), A("u7"), 1.0 / W, AL.mult)
+        ts(A("nw"), A("pr"), 5, AL.arith_shift_right, W - 1, AL.bitwise_and)
+        cp(c("NEW", 0, 16), A("nw"))
+        cp(c("NEW", 16, 32), A("nw"))
+        for j in range(0, n, 32):
+            mm(c("P6", j, min(j + 32, n)), A("IH"), c("NEW", 0, min(32, n - j)), False, j + 32 >= n)
+        tt(A("CF"), A("c1"), A("BC"), AL.add)
+        tt(hs("E", 0, 32), st(t, 0, 4), lst(t, 0, 4), AL.is_equal)
+        tt(hs("E", 32, 40), st(t, 2), lst(t, 3), AL.is_equal)
+        tt(hs("E", 40, 48), st(t, 3), lst(t, 2), AL.is_equal)
+        tt(c("DL", 0, n), c("P6", 0, n), c("EQ", 0, n), AL.mult)
+        if not last:
+            mm(c("P7", 0, n), A("IH"), c("DL", 0, n), False, True)
+        tt(hs("E", 8, 16), hs("E", 0, 8), hs("E", 8, 16), AL.mult)
+        tt(A("HK"), A("uh"), A("K"), AL.mult)
+        tt(A("LM"), hs("E", 8, 48), A(lim), AL.mult)
+        tt(A("K2"), A("gk"), A("K"), AL.mult)
+        if not last:
+            hash_tail(c("P7", 0, n), t + 1)
+        mm(DN[far], A("NI"), pn("L1", far), False, True)
+        act(c("AN", 128 * far, 128 * far + 128), DN[far], AF.Abs)
+        if t:
+            mm(c("P6", 256, 256 + m), A("IF"), c("TT", 0, m), True, False)
+            mm(c("P6", 256, 256 + m), A("IH"), c("DK", 0, m), False, True)
+
+        mm(DN[near], A("NI"), pn("L1", near), False, True)
+        act(c("AN", 128 * near, 128 * near + 128), DN[near], AF.Abs)
+        if t:
+            act(c("TT", 0, m), c("P6", 256, 256 + m), AF.Copy)
+        rows(c("P3", 0, 16), "SEL", lambda p: A("AN", S_[:, p::16]))
+        tt(A("bad"), c("P3", 0, 16), hs("LM", 0, 8), AL.is_ge)
+        tt(A("ok"), c("P3", 0, 16), hs("LM", 0, 8), AL.is_lt)
+        tt(A("sy"), A("bad"), A("CF"), AL.add)
+        ts(A("SO"), A("sy"), float(W), AL.mult)
+        tt(X(A("X"), A("SO")), A("VAL"), A("C192"), AL.add)
+        if last:
+            dma("y", A("yx"), XT)
+
+        for h in range(2):
+            P = "P%d" % (1 + h)
+            mm(c(P, 0, 256), A("NI"), A("L2", S_[:, t, h, :]), False, True)
+            mm(c(P, 256, 512), A("ID"), A("S2", S_[:, t, h, :]), True, False)
+            mm(c(P, 256, 384), A("NI"), A("L2", S_[:, t, h, 128:256]), False, False)
+            mm(c(P, 384, 512), A("NI"), A("L2", S_[:, t, h, 0:128]), False, True)
+            act(c("AR", 512 * h, 512 * h + 512), A(P), AF.Abs)
+        for j in range(L):
+            mm(c("P5", 16 * j, 16 * j + 16), A("ID"), A("ok"), True, True)
+        rows(c("P4", 0, 64), "SEL", lambda p: A("AR", S_[:, p::16]))
+        if not last:
+            for j in range(NE[t + 1]):
+                gather("v", t + 1, j, None)
+        else:
+            tt(c("DK", 0, n), c("DL", 0, n), c("P5", 0, n), AL.mult)
+            mm(c("P6", 256, 256 + n), A("IF"), c("TT", 0, n), True, False)
+            mm(c("P6", 256, 256 + n), A("IH"), c("DK", 0, n), False, True)
+            act(A("YT"), c("P6", 256, 256 + n), AF.Identity, -32.0)
+            dma("y", A("yt"), A("YT"))
+            tt(A("kv"), A("bad"), A("nf"), AL.mult)
+        tt(A("wn"), st(t, 1), A("ok"), AL.add)
+        tt(A("AG"), c("P4", 0, 64), hs("LM", 8, 40), AL.is_lt)
+        tt(A("av"), hs("AG", 0, 16), hs("AG", 16, 32), AL.max)
+        tt(A("cv"), A("V"), A("av"), AL.add)
+        tt(A("PT", S_[:, :, 0, :]), hs("cv", 0, 8), A("HK"), AL.is_ge)
+        tt(A("PT", S_[:, :, 1, :]), hs("cv", 8, 16), A("HK"), AL.is_ge)
+        if last:
+            tt(c("YS", 32, 48), hs("cv", 0, 8), A("kv"), AL.mult)
+        tt(A("PT", S_[:, :, 2:4, :]), A("PT", S_[:, :, 0:2, :]), st(t, 2, 4), AL.mult)
+        if last:
+            tt(c("YS", 48, 64), hs("cv", 8, 16), A("kv"), AL.mult)
+        tt(A("RQ"), A("PT", S_[:, :, 0::2, :]), A("PT", S_[:, :, 1::2, :]), AL.max)
+        rw, qq = A("RQ", S_[:, :, 0, :]), A("RQ", S_[:, :, 1, :])
+        tt(A("keep"), rw, A("ok"), AL.is_le)
+        tt(A("nor"), A("bad"), rw, AL.is_gt)
+        tt(A("xn"), A("keep"), A("wn"), AL.mult)
+        if last:
+            tt(A("t0"), A("nor"), A("ek"), AL.mult)
+            tt(A("zz"), qq, A("xn"), AL.max)
+            ts(c("YS", 16, 32), A("t0"), 0.5, AL.max, 2.0, AL.mult)
+            ts(c("YS", 0, 16), A("zz"), -0.25, AL.add)
+            dma("s", A("yst"), A("YS"))
+        else:
+            tt(A("t1"), A("nor"), A("K2"), AL.mult)
+            tt(st(t + 1, 1), qq, A("xn"), AL.max)
+            rounders("t1")
+            ts(A("K"), A("t1"), 1.0, AL.max)
+            tt(A("t0"), A("nor"), A("ek"), AL.mult)
+            mm(c("P4", 64, 80), A("ON"), A("keep"), True, True)
+            points_of(t + 1)
+            ts(st(t + 1, 0), A("t0"), 0.5, AL.max)
+
+    for sem, val in cnt.items():
+        wait("g", sem, val)

@@ -5,6 +5,11 @@ from concourse.mybir import AluOpType, ActivationFunctionType
 RO, TOP, SLOTS, W = 5, 9, 14, 2048
 PM = (1, 4)
 F, B, I, U, H = "float32", "bfloat16", "int32", "uint16", "float16"
+QV1, QV2, QT1, QT2, QKEEP, QK, QKK = 0, 2, 4, 6, 8, 10, 12
+QNN, QM2, QG, QN, QM1 = 5, 7, 9, 11, 13
+QP, QP1, QP2, QEND = 14, 30, 46, 62
+SCALES = {"ID": 1.0, "NI": -1.0, "I16": 16.0, "NH": -0.5, "N15": -1.5, "N31": -31.0, "CP": 1.125 * 2.0 ** 24,
+          "CN": -1.125 * 2.0 ** 24, "I1184": 1184.0, "N16": -16.0, "I2": 2.0, "I4": 4.0, "NS": -1.0 / 8, "N2K": -2048.0}
 
 
 def _sb(n, d):
@@ -12,39 +17,36 @@ def _sb(n, d):
 
 
 SCRATCH = {
-    "X": _sb(2 * W, B), "G": _sb(256 * 14, B), "R": _sb(256 * 14, B), "ZE": _sb(128 * 14, B),
-    "S1": _sb([RO, 2, 160], B), "L1": _sb([RO, 2, 160], B), "S2": _sb([RO, 2, 256], B), "L2": _sb([RO, 2, 256], B),
+    "X": _sb(3 * W, B), "G": _sb(256 * 13, B), "R": _sb(256 * 13, B), "GN": _sb(256, B),
+    "y0": _sb(16, F), "y1": _sb(16, F), "yn": _sb(16, I), "yc": _sb(16, I), "CN16": _sb(16, H), "GO": _sb(16, U), "T0": _sb(224, F),
+    "S1": _sb([RO + 1, 2, 8 * QEND], B), "L1": _sb([RO, 2, 8 * QEND], B),
     "tri": _sb(224, I), "sdi": _sb(80, I), "n0i": _sb(16, I), "k0i": _sb(16, I), "thi": _sb(16, I), "wti": _sb(1, I),
-    "TT": _sb(224, F), "S32": _sb(80, F), "SR": _sb(224, F), "DL": _sb(224, H), "DK": _sb(224, H), "EQ": _sb(224, F),
-    "IF": _sb(128, F), "NF": _sb(128, F), "IH": _sb(128, H), "NH": _sb(128, H), "C32": _sb(224, B),
-    "EA": _sb(224, F), "YI": _sb(224, I), "YB": _sb(224, I), "CI": _sb(224, U), "BE": _sb(224, F), "JC": _sb(224, B),
-    "IC": _sb(144, F), "SEL": _sb(144, B), "WM": _sb(144, H), "ID": _sb(128, B), "NI": _sb(128, B), "ON": _sb(128, B),
+    "TS": _sb(224, F), "SD": _sb(80, H), "EA": _sb(224, B), "C32": _sb(224, B), "C2080": _sb(224, B),
+    "YI": _sb(224, I), "YB": _sb(224, I), "CI": _sb(224, U), "BE": _sb(224, F), "JC": _sb(224, B),
+    "IC": _sb(144, F), "SEL": _sb(144, B), "WM": _sb(144, H), "ON": _sb(224, B), "OP": _sb(128, F), "OM": _sb(128, F),
     "pi": _sb(1, I), "pa": _sb(1, I), "pb": _sb(1, I), "pf": _sb(1, F), "gf": _sb(1, F), "pm": _sb(1, F),
-    "wa": _sb(1, I), "wb": _sb(1, I), "wf": _sb(1, F),
-    "REP": _sb(16, U), "IA": _sb(16, F), "IB": _sb(48, F), "IL": _sb(48, F), "BC": _sb(16, F), "OB": _sb(48, F),
-    "OF": _sb(48, F), "OU": _sb(48, U), "THR": _sb([2, 40], F), "LI": _sb([2, 40], F), "E": _sb([2, 48], F),
-    "LM": _sb([2, 40], F), "AN": _sb(256, B), "AR": _sb(1024, B), "VAL": _sb(256, B), "C192": _sb(256, B),
-    "ui": _sb(16, I), "uu": _sb(16, I), "u7": _sb(16, I), "w1": _sb(16, F), "w2": _sb(16, F), "pr": _sb(16, I), "nw": _sb(16, I),
-    "NEW": _sb(32, H), "c1": _sb(16, F), "CF": _sb(16, F), "bad": _sb(16, F), "sy": _sb(16, F), "SO": _sb(16, U),
-    "ok": _sb(16, B), "AG": _sb([2, 32], F), "av": _sb([2, 16], F), "cv": _sb([2, 16], F), "V": _sb([2, 16], F),
-    "PT": _sb([2, 4, 8], F), "RQ": _sb([2, 2, 8], F), "keep": _sb(16, B), "wn": _sb(16, F), "xn": _sb(16, F), "nor": _sb(16, F),
-    "t0": _sb(16, F), "t1": _sb(16, F), "K": _sb(16, F), "CC": _sb(16, F), "BB": _sb(16, F), "zz": _sb(16, F),
-    "MR": _sb([2, 16], F), "ek": _sb(16, F), "nf": _sb(16, F), "uh": _sb(16, F), "HK": _sb(16, F), "gk": _sb(16, F),
-    "K2": _sb(16, F), "kv": _sb(16, F), "b2": _sb(16, F), "b4": _sb(16, F), "b8": _sb(16, F),
-    "aj": _sb(16, F), "nx": _sb(1, F), "r1": _sb(1, F), "r2": _sb(1, F), "r3": _sb(1, F), "a15": _sb(1, F),
-    "YS": _sb(64, F), "YT": _sb(224, F),
+    "wa": _sb(1, I), "wb": _sb(1, I), "wf": _sb(1, F), "K2K": _sb(16, B), "K35": _sb(8, B), "K27": _sb(1, B), "K75": _sb(1, B),
+    "IA": _sb(16, F), "IB": _sb(48, F), "IL": _sb(48, F), "BC": _sb(16, F), "OB": _sb([RO, 48], H), "OU": _sb(48, U),
+    "TH": _sb([2, 4, 8], F), "LI": _sb([2, 4, 8], H), "EV": _sb([2, 4, 8], B), "AG": _sb([2, 4, 8], B), "BB": _sb([2, 2, 8], B),
+    "AN": _sb([2, 144], B), "AR": _sb(1024, B), "VAL": _sb(256, B), "C192": _sb(128, B),
+    "ui": _sb(16, I), "uu": _sb(16, I), "u7": _sb(16, I), "w2": _sb(16, F), "pr": _sb(16, I), "nw": _sb(16, I),
+    "NEW": _sb(16, H), "CF": _sb(16, H), "SO": _sb(16, U), "ok": _sb(16, B), "N0": _sb(16, B),
+    "b2": _sb(16, F), "b4": _sb(16, F), "b8": _sb(16, F), "t0": _sb(16, F), "aj": _sb(16, F), "nx": _sb(1, F),
+    "YS": _sb([4, 2, 8], F), "YT": _sb(224, F),
 }
+for _n in SCALES:
+    SCRATCH[_n] = _sb(128, B)
 for _i in range(8):
-    SCRATCH["P%d" % _i] = ("psum", [128, 512], F)
+    SCRATCH["P%d" % _i] = ("psum", [128, 2, 32, 8], F)
 
 SEMAPHORES = (["cv_", "cs_", "ct_", "cg_", "loc"] + ["d%d" % i for i in range(10)]
-              + ["a%d_%d" % (t, h) for t in range(RO) for h in range(2)]
-              + ["b%d" % t for t in range(RO)] + ["c%d" % t for t in range(RO)])
+              + ["%s%d" % (n, t) for t in range(RO) for n in "abce"])
 
-NV = [3, 2, 3, 3, 3]
-NE = [0, 2, 2, 2, 2]
-ND = [3, 4, 4, 4, 4]
-BIG = 1.5 * 2.0 ** 23
+NV = [4, 3, 4, 4, 4]
+ND = [3, 3, 3, 4, 4]
+ORDER = """s s s v AG s s s s v s L2 v L3 v L4 s be scanF s OU S V nF a A scanN nN b seeds EA bnd 1F 2F c 2N 1N e G0
+    LI u min ownF ui uu ptsF ptsN len0 u7 ownN max w2 pr dnF h0 CF h1 nw Z0 T0 decF y1 NEW dnN yn h2 VAL len yc EV soF
+    dpF h3 decN cn wrF soN ok dpN e4n wrN e2 e3 Z2 GO sums Z1 eok""".split()
 AL = AluOpType
 AF = ActivationFunctionType
 S_ = np.s_
@@ -169,8 +171,17 @@ def rank_program(g, core, T, topo):
         else:
             emit("s", lambda: g.scalar.activation(ap(o), ap(a), fn, ap(bias), scale), [o], [a, bias])
 
-    def mm(o, l, r, st, sp):
-        emit("t", lambda: g.tensor.matmul(ap(o), ap(l), ap(r), st, sp), [o], [l, r])
+    opened = {}
+
+    def mm(o, l, r, stop=False):
+        l = A(l) if isinstance(l, str) else l
+        start = not opened.get(o[0])
+        opened[o[0]] = not stop
+        emit("t", lambda: g.tensor.matmul(ap(o), ap(l), ap(r), start, stop), [o], [l, r])
+
+    def mms(terms, stop=False):
+        for i, (o, l, r) in enumerate(terms):
+            mm(o, l, r, stop and i == len(terms) - 1)
 
     def iota(o, pat, base, cm):
         if SCRATCH[o[0]][2] == I:
@@ -193,45 +204,60 @@ def rank_program(g, core, T, topo):
     near = 1 - far
     eng[near] = [e for e in eng[near] if e not in eng[far]]
     msk = [sum(1 << e for e in es) for es in eng]
-    total = len(eng[0]) + len(eng[1])
     dst = []
     for m in mate:
         rid, pid = topo.addr(m, core)
         dst.append(DstId(rid=rid, pnc=pid))
+    MSG = {"a": (far, QK, QP1), "b": (near, QK, QP1), "c": (far, QP1, QEND), "e": (near, QP1, QEND)}
     for t in range(RO):
-        for h in range(2):
-            mark(A("L1", S_[:, t, h, 32:160]), "a%d_%d" % (t, h), len(eng[h]))
-        mark(A("L1", S_[:, t, :, 0:32]), "c%d" % t, total)
-        mark(A("L2", S_[:, t]), "b%d" % t, total)
+        for nm, (h, a, b) in MSG.items():
+            mark(A("L1", S_[:, t, h, 8 * a:8 * b]), "%s%d" % (nm, t), len(eng[h]))
 
-    def send(src, land, sem, t, halves, a, b):
-        cnt["loc"] = cnt.get("loc", 0) + sum(len(eng[h]) for h in halves)
-        order("g", [A(src, S_[:, t, h, a:b]) for h in halves], [], "loc", cnt["loc"])
-        g.remote_dma_fused([RemoteDMATransfer(dst_ids=[dst[h]], dma_engine_mask=msk[h], remote_sem=T.sem[sem],
-                                              src=T[src][:, t, h, a:b], dst=T[land][:, t, h, a:b]) for h in halves],
+    def send(nm, t):
+        h, a, b = MSG[nm]
+        cnt["loc"] = cnt.get("loc", 0) + len(eng[h])
+        order("g", [A("S1", S_[:, t, h, 8 * a:8 * b])], [], "loc", cnt["loc"])
+        g.remote_dma_fused([RemoteDMATransfer(dst_ids=[dst[h]], dma_engine_mask=msk[h], remote_sem=T.sem["%s%d" % (nm, t)],
+                                              src=T["S1"][:, t, h, 8 * a:8 * b], dst=T["L1"][:, t, h, 8 * a:8 * b])],
                            local_sem=T.sem["loc"])
 
-    def st(t, a, b=None):
-        return A("S1", S_[:, t, :, 8 * a:8 * (a + 1 if b is None else b)])
+    def sl(a, b, s):
+        return a if b is None else slice(a, b, s)
 
-    def lst(t, a, b=None):
-        return A("L1", S_[:, t, :, 8 * a:8 * (a + 1 if b is None else b)])
+    def st(t, a, b=None, s=1, h=None, nm="S1"):
+        if b is not None and s == 1:
+            cols = slice(8 * a, 8 * b)
+        else:
+            cols = slice(16 * (a // 2) + a % 2, 16 * ((a if b is None else b - 1) // 2) + 16, 2)
+        return A(nm, S_[:, t, sl(0, 2, 1) if h is None else h, cols])
+
+    def lst(t, a, b=None, h=None):
+        return st(t, a, b, 1, h, "L1")
+
+    def ps(k, a, b=None, s=1, h=None):
+        return A("P%d" % k, S_[:, sl(0, 2, 1) if h is None else h, sl(a, b, s), :])
+
+    def pf(k, h, a, b):
+        return ps(k, a // 8, b // 8, 1, h)
+
+    def q3(nm, a, b=None, h=None):
+        return A(nm, S_[:, sl(0, 2, 1) if h is None else h, sl(a, b, 1), :])
 
     def c(nm, a, b):
         return A(nm, S_[:, a:b])
 
-    def hs(nm, a, b):
-        return A(nm, S_[:, :, a:b])
-
     XT = c("X", 0, W)
+    ON16, OK = c("ON", 0, 16), A("ok")
+    DN = {far: 0, near: 1}
+    DV = {far: 2, near: 3}
 
     dma("y", A("tri"), A("tr"))
     dma("s", A("sdi"), A("sd"))
-    dma("y", XT, A("xt"))
     dma("s", A("k0i"), A("k0"))
-    dma("s", A("n0i"), A("n0"))
+    dma("y", A("n0i"), A("n0"))
     dma("s", A("wti"), A("wt"))
-    dma("s", A("thi"), A("th"))
+    dma("y", A("thi"), A("th"))
+    dma("y", XT, A("xt"))
     iota(A("pi"), [[0, 1]], 0, 1)
     iota(A("IC"), [[1, 144]], 0, 0)
     iota(A("BE"), [[1184, SLOTS], [0, 16]], -1024, 0)
@@ -239,78 +265,79 @@ def rank_program(g, core, T, topo):
     iota(A("IA"), [[16, 16]], 0, 0)
     iota(A("G", S_[:, 0:256 * (TOP + 1):TOP + 1]), [[0, 256]], -256, 0)
     iota(A("JC"), [[1, SLOTS], [0, 16]], 0, 0)
-    fill(A("ZE"), 0.0)
+    fill(A("C2080"), 2080.0)
+    fill(A("ON"), 1.0)
+    cp(A("pf"), A("pi"))
+    fill(A("C32"), 32.0)
     ts(A("pa"), A("pi"), 15, AL.bitwise_and)
     ts(A("pb"), A("pi"), 112, AL.bitwise_and)
-    cp(A("pf"), A("pi"))
+    ts(A("ID"), c("IC", 0, 128), A("pf"), AL.is_equal)
     cp(A("pm"), A("pa"))
     ts(A("gf"), A("pb"), 15.0, AL.add)
-    ts(A("REP"), c("ZE", 0, 16), A("pm"), AL.add)
-    ts(A("ID"), c("IC", 0, 128), A("pf"), AL.is_equal)
-    act(A("NI"), A("ID"), AF.Identity, 0.0, -1.0)
-    act(A("IF"), A("ID"), AF.Copy)
-    act(A("NF"), A("ID"), AF.Identity, 0.0, -1.0)
-    ts(A("SEL"), A("IC"), A("gf"), AL.is_equal)
-    ts(A("IH"), c("IC", 0, 128), A("pf"), AL.is_equal)
-    ts(A("NH"), c("IC", 0, 128), A("pf"), AL.is_equal, -1.0, AL.mult)
-    fill(A("C32"), 32.0)
-    fill(A("C192"), -192.0)
-    fill(A("ON"), 1.0)
-    fill(A("V"), 0.0)
+    fill(c("X", W, 2 * W), 0.0)
+    for nm in list(SCALES)[1:]:
+        act(A(nm), A("ID"), AF.Identity, 0.0, SCALES[nm])
     ts(A("IL"), A("IB"), A("pm"), AL.add)
-    ts(A("BC"), A("IA"), A("pm"), AL.add, 8.0 / W, AL.mult)
+    ts(A("SEL"), A("IC"), A("gf"), AL.is_equal, 1.0 / 8, AL.mult)
 
-    def rep_seed(t):
-        k = TOP + t
-        act(c("SR", 0, 16 * k), X(c("S32", 16 * t, 16 * t + 16), c("REP", 0, k)), AF.Copy)
+    def steps(t):
+        return TOP + max(t - 1, 0)
 
-    def hash_tail(src, t):
-        n = 16 * (TOP + t)
-        tt(c("P7", 256, 256 + n), src, c("SR", 0, n), AL.mult)
-        tt(c("YI", 0, n), c("P7", 256, 256 + n), c("BE", 0, n), AL.add)
-        ts(c("YB", 0, n), c("YI", 0, n), 5, AL.logical_shift_right, W - 1, AL.bitwise_and)
-        cp(c("CI", 0, n), c("YB", 0, n))
+    def seeds(t):
+        k = steps(t)
+        mms([(pf(7, 0, 0, 16 * k), "ID", c("C2080", 0, 16 * k))]
+            + [(pf(7, 0, 16 * j, 16 * j + 16), "ID", c("SD", 16 * t, 16 * t + 16)) for j in range(k)], True)
 
-    def rounders(src):
-        ts(A("CC"), A(src), 1.0, AL.max, 2.0 ** 23 - 0.5, AL.mult)
-        ts(A("BB"), A(src), 1.0, AL.max, 2.0 ** 23, AL.mult)
+    def hashed(t):
+        n = 16 * steps(t)
+        return [lambda: tt(pf(7, 1, 0, n), c("TS", 0, n), pf(7, 0, 0, n), AL.mult),
+                lambda: tt(c("YI", 0, n), pf(7, 1, 0, n), c("BE", 0, n), AL.add),
+                lambda: ts(c("YB", 0, n), c("YI", 0, n), 5, AL.logical_shift_right, W - 1, AL.bitwise_and),
+                lambda: cp(c("CI", 0, n), c("YB", 0, n))]
 
-    def points_of(t):
-        tt(A("zz"), st(t, 1), A("CC"), AL.add)
-        tt(hs("MR", 0, 8), A("zz"), A("BB"), AL.subtract)
-        tt(hs("MR", 8, 16), hs("MR", 0, 8), A("K"), AL.subtract)
-        ts(st(t, 2, 4), A("MR"), 0.0, AL.max, 0.25, AL.add)
-        tt(A("OF"), st(t, 1, 4), A("OB"), AL.add)
-        cp(A("OU"), A("OF"))
+    h0 = hashed(0)
+    ts(A("SD"), A("sdi"), -2048.0, AL.add)
+    ts(A("TS"), A("tri"), 32.0, AL.add)
+    seeds(0)
+    ts(A("b2"), A("k0i"), 2.0, AL.is_ge)
+    ts(A("b4"), A("k0i"), 4.0, AL.is_ge, 3.0, AL.mult)
+    h0[0]()
+    ts(A("b8"), A("k0i"), 8.0, AL.is_ge, 7.0, AL.mult)
+    tt(A("t0"), A("b2"), A("b4"), AL.max)
+    h0[1]()
+    ts(st(0, QK), A("k0i"), -1.0, AL.add)
+    tt(st(0, QKK), A("t0"), A("b8"), AL.max)
+    h0[2]()
+    cp(A("N0"), A("n0i"))
+    ts(st(0, QV1, QV2 + 1, 2), c("ON", 0, 32), 0.0, AL.mult)
+    h0[3]()
+    for t in range(RO):
+        act(A("OB", S_[:, t]), A("IL"), AF.Identity, 0.0, float(steps(t) + 1))
+    act(A("OP"), c("ON", 0, 128), AF.Identity, 0.0, 1.0 / 16)
+    act(A("OM"), c("ON", 0, 128), AF.Identity, 0.0, -1.0 / 16)
+    for nm, n, v in (("K27", 1, 1.5 * 2.0 ** 27), ("K75", 1, 7.5), ("K2K", 16, 2048.0), ("K35", 8, 1.5 * 2.0 ** 35), ("C192", 128, -192.0)):
+        act(A(nm), c("ON", 0, n), AF.Identity, 0.0, v)
 
-    ts(A("S32"), A("sdi"), 32.0, AL.add)
-    ts(A("TT"), A("tri"), 32.0, AL.add)
-    rep_seed(0)
-    act(A("OB"), A("IL"), AF.Identity, -0.25, float(TOP + 1))
-    hash_tail(c("TT", 0, 16 * TOP), 0)
-
-    def first_state():
-        ts(A("b2"), A("k0i"), 2.0, AL.is_ge, 1.0, AL.add)
-        ts(A("b4"), A("k0i"), 4.0, AL.is_ge, 4.0, AL.mult)
-        ts(A("b8"), A("k0i"), 8.0, AL.is_ge, 8.0, AL.mult)
-        tt(A("t0"), A("b2"), A("b4"), AL.max)
-        ts(st(0, 1), A("n0i"), 0.25, AL.add)
-        tt(A("K"), A("t0"), A("b8"), AL.max)
-        ts(st(0, 0), A("k0i"), 0.5, AL.mult)
-        rounders("K")
-        points_of(0)
+    def weights():
         ts(A("wa"), A("wti"), 2048.0, AL.add)
-        ts(hs("THR", 0, 8), A("thi"), 1.0, AL.add)
+        ts(q3("TH", 0), A("thi"), 0.5, AL.add)
         ts(A("wb"), A("wa"), 4095, AL.bitwise_and)
+        ts(A("BC"), A("IA"), A("pm"), AL.add, 8.0, AL.mult)
         ts(A("wf"), A("wb"), -2048.0, AL.add)
+
+    def weights2():
         ts(A("WM"), A("IC"), A("gf"), AL.is_equal, A("wf"), AL.mult)
 
-    def rows(o, mat, src):
-        for p in range(16):
-            mm(o, c(mat, 15 - p, 143 - p), src(p), p == 0, p == 15)
+    def thresholds():
+        for k in range(1, 4):
+            act(q3("TH", k), q3("TH", 0), AF.Copy)
+        act(A("LI"), A("TH"), AF.Copy)
 
     def gather(q, t, j, h):
-        L = TOP + t + 1
+        L = steps(t) + 1
+        if j is None:
+            act(A("GN"), X(c("X", 0, 2 * W), A("GO")), AF.Copy)
+            return
         if h is None:
             o, off = A("G", S_[:, 1 + j:256 * L:L]), c("CI", 16 * j, 16 * j + 16)
         else:
@@ -320,185 +347,234 @@ def rank_program(g, core, T, topo):
         else:
             act(o, X(XT, off), AF.Copy)
 
-    for t in range(RO):
-        J = TOP + t
+    def early2(t):
+        mms([(ps(7, 0, 2), "I2", st(t, QV1, QV2 + 1, 2))]
+            + [(ps(7, k), m, st(t, r)) for k in range(2) for m, r in (("N31", QKK), ("I16", QK), ("NI", QK))])
+
+    def early3(t):
+        n, m1, m2, gg = [st(t, q) for q in (QN, QM1, QM2, QG)]
+        mms([(ps(0, 2, 4), "N16", c("ON", 0, 32)), (ps(0, 4), "I16", ON16), (ps(0, 5), "ID", ON16),
+             (ps(0, 0, 2), "ID", st(t, QV1, QV2 + 1, 2)),
+             (ps(0, 6), "ID", gg), (ps(0, 5, 7), "ID", st(t, QK, QKK + 1, 2)), (ps(0, 2), "NI", m1), (ps(0, 3), "NI", m2)]
+            + [(ps(0, k), "N16", gg) for k in (0, 1)] + [(ps(0, k), "ID", n) for k in (2, 3)])
+
+    def early4(n):
+        mms([(ps(1, 0), "I16", ON16), (ps(1, 1), "NI", ON16), (ps(1, 2), "ID", ON16)] + [(ps(1, k), "ID", n) for k in (0, 1, 3, 4)])
+
+    def appended(t):
+        mms([(ps(7, k), "N16", OK) for k in (0, 1)] + [(ps(0, k), "N16", OK) for k in (0, 1, 5, 6)])
+        if t < RO - 1:
+            mms([(ps(1, 0), "N16", OK)] + [(ps(1, k), "ID", OK) for k in (1, 3, 4)])
+        else:
+            mms([(ps(1, 0), "ID", st(t, QN)), (ps(1, 0), "ID", OK), (ps(1, 1), "ID", ON16)])
+
+    def lengths(t, own):
+        q1, qK = lst(t, QM1), lst(t, QKK)
+        mms([(ps(4, 9, 12, 2), "I16", c("ON", 0, 32))] + [(ps(4, k), "I16", st(t, QM1)) for k in (8, 11)]
+            + [(ps(4, k), "I16", st(t, QM2)) for k in (9, 10)] if own else
+            [(ps(4, k), "N16", q1) for k in (8, 9, 10, 11)] + [(ps(4, k), "I16", qK) for k in (9, 11)], not own)
+
+    def sums(t):
+        mms([(ps(4, 0, 4), "NS", A("LI"))] + [(ps(4, 0, 4), c("SEL", 15 - p, 143 - p), A("AR", S_[:, p::16])) for p in range(16)]
+            + [(ps(4, 0, 4), "I4", A("EV"))], True)
+
+    def counted(k, m, stop):
+        mms([(ps(k, 0, 2), m, q3("AG", 0, 2)), (ps(k, 0), m, q3("AG", 3)), (ps(k, 1), m, q3("AG", 2))], stop)
+
+    def layer2(t):
+        counted(7, "I2", True)
+        counted(0, "ID", False)
+        ts(A("BB"), ps(7, 0, 2), 1.0, AL.is_ge)
+
+    def layer3(t):
+        b1, b2 = q3("BB", 0), q3("BB", 1)
+        mms([(ps(0, 2), "I16", b1), (ps(0, 3), "I16", b2)] + [(ps(0, k), "N16", b1) for k in (3, 4, 5, 6)]
+            + [(ps(0, k), "N16", b2) for k in (4, 5, 6)], True)
+        ts(st(t + 1, QV1, QKK + 1, 2), ps(0, 0, 7), 0.0, AL.max)
+
+    def layer4(t):
+        KK, kk, t1, t2 = [st(t, q) for q in (QKK, QK, QT1, QT2)]
+        if t:
+            mms([(ps(1, 3, 5), "NI", st(t, QT1, QT2 + 1, 2)), (ps(1, 3), "NI", t2), (ps(1, 4), "NI", t1),
+                 (ps(1, 1), "NI", t1), (ps(1, 1), "NI", t2)])
+        mms([(ps(1, 1), "N15", KK), (ps(1, 4), "NH", KK), (ps(1, 2), "N31", KK), (ps(1, 2), "I16", kk)]
+            + [(ps(1, k), m, KK) for m in ("CP", "CN") for k in (1, 4)], True)
+        ts(st(t, QNN, QM1 + 1, 2), ps(1, 0, 5), 0.0, AL.max)
+
+    def places(t):
+        mms([(ps(5, 0, 3), "ID", A("OB", S_[:, t]))] + [(ps(5, k), "NI", OK) for k in ((0, 1) if t else ())]
+            + [(ps(5, 0, 2), "ID", st(t, QN, QM1 + 1, 2)), (ps(5, 2), "ID", st(t, QM2))], True)
+        cp(A("OU"), ps(5, 0, 3))
+
+    def limits():
+        o = A("P3", S_[:, 0, 31, 0:1])
+        mms([(o, "OP", A("nx")), (o, "ID", A("K75")), (o, "ID", A("K27")), (o, "NI", A("K27")), (o, "OM", A("nx"))], True)
+        ts(A("LI"), A("TH"), o, AL.add)
+
+    def slot(n, at):
+        mms([(pf(6, 0, 0, n), "NI", c("JC", 0, n))] + [(pf(6, 0, j, j + 16), "ID", at) for j in range(0, n, 16)], True)
+        act(c("EA", 0, n), pf(6, 0, 0, n), AF.Abs, 0.0, 4096.0)
+
+    def bounds(n):
+        mms([(pf(6, 1, 0, n), "ID", c("EA", 0, n)), (pf(6, 0, 0, n), "NI", c("EA", 0, n)), (pf(6, 0, 0, n), "ID", c("C32", 0, n))]
+            + [(pf(6, 0, j, j + 16), "ID", A("NEW")) for j in range(0, n, 16)], True)
+
+    def last_slot(k):
+        n = 16 * SLOTS
+        every = range(0, n, 16)
+        if k == 0:
+            mms([(pf(6, 0, 0, n), "NI", A("JC")), (pf(6, 0, 0, n), "I16", A("ON"))]
+                + [(pf(6, 0, j, j + 16), "ID", st(RO - 1, QN)) for j in every])
+        elif k == 1:
+            mms([(pf(6, 0, j, j + 16), "N16", OK) for j in every], True)
+            act(A("EA"), pf(6, 0, 0, n), AF.Abs, 0.0, 4096.0)
+        else:
+            mms([(pf(2, 0, j, j + 16), "ID", A("NEW")) for j in every])
+
+    def one_round(t):
+        J = steps(t)
         L = J + 1
-        n = 16 * L
+        m = 16 * (TOP + t)
         last = t == RO - 1
 
         def win(nm, h):
             return c(nm, 128 * L * h, 128 * L * (h + 1))
 
         def scan(h):
-            o, d0, d1 = win("R", h), win("G", h), c("ZE", 0, 128 * L)
+            o, d0, d1 = win("R", h), win("G", h), c("X", W, W + 128 * L)
             emit("v", lambda: g.vector.tensor_tensor_scan(ap(o), ap(d0), ap(d1), 0.0, AL.add, AL.max), [o], [d0, d1])
 
-        def pn(nm, h):
-            return A(nm, S_[:, t, h, 32:160])
+        def pick(k, h):
+            o, src = st(t, QP + 16 * k, QP + 16 * k + 16, 1, h), X(win("R", h), c("OU", 24 * h + 8 * k, 24 * h + 8 * k + 8))
+            if k == 2:
+                act(o, src, AF.Copy)
+            elif t:
+                tt(o, src, c("GN", 128 * h, 128 * h + 128), AL.add)
+            else:
+                cp(o, src)
 
-        nv, ndf = NV[t], ND[t]
-        for j in range(nv, J - ndf):
-            gather("s", t, j, None)
-        for h in (far, near):
-            for j in range(J - ndf, J):
-                gather("s", t, j, h)
-        if t == 0:
-            first_state()
-        for j in range(NE[t], nv):
-            gather("v", t, j, None)
-        mm(c("P0", 256, 256 + n), A("NI"), c("JC", 0, n), True, False)
-        for j in range(L):
-            mm(c("P0", 256 + 16 * j, 272 + 16 * j), A("ID"), st(t, 1), False, j == L - 1)
-        mm(c("P6", 0, n), A("NF"), c("TT", 0, n), True, False)
-        mm(c("P6", 0, n), A("ID"), c("C32", 0, n), False, False)
-        if not last:
-            mm(c("P7", 0, n), A("IF"), c("TT", 0, n), True, False)
-        send("S1", "L1", "c%d" % t, t, [0, 1], 0, 32)
-        scan(far)
-        act(pn("S1", far), X(win("R", far), c("OU", 24 * far, 24 * far + 8)), AF.Copy)
-        send("S1", "L1", "a%d_%d" % (t, far), t, [far], 32, 160)
-        act(A("S2", S_[:, t, far, :]), X(win("R", far), c("OU", 24 * far + 8, 24 * far + 24)), AF.Copy)
-        scan(near)
-        cp(pn("S1", near), X(win("R", near), c("OU", 24 * near, 24 * near + 8)))
-        send("S1", "L1", "a%d_%d" % (t, near), t, [near], 32, 160)
-        act(A("S2", S_[:, t, near, :]), X(win("R", near), c("OU", 24 * near + 8, 24 * near + 24)), AF.Copy)
-        send("S2", "L2", "b%d" % t, t, [0, 1], 0, 256)
-        if not last:
-            iota(A("G", S_[:, 0:256 * (L + 1):L + 1]), [[0, 256]], -256, 0)
+        def own_n(h):
+            mms([(pf(DN[h], 0, 0, 128), "ID", st(t, QP, QP1, 1, h)), (pf(DN[h], 0, 128, 144), "I16", st(t, QK, QN + 1, 1, h))])
 
-        PN = A("S1", S_[:, t, :, 32:160])
-        rows(c("P3", 16, 32), "WM", lambda p: A("S1", S_[:, t, :, 32 + p:160:16]))
-        act(c("EA", 0, n), c("P0", 256, 256 + n), AF.Abs, -0.25)
-        if t:
-            m = n - 16
-            tt(c("DK", 0, m), c("DL", 0, m), c("P5", 0, m), AL.mult)
-            mm(c("P6", 0, m), A("NH"), c("DK", 0, m), False, False)
-            if not last:
-                mm(c("P7", 0, m), A("IH"), c("DK", 0, m), False, False)
-            tt(A("kv"), A("bad"), A("nf"), AL.mult)
-            tt(hs("V", 0, 8), hs("cv", 0, 8), A("kv"), AL.mult)
-            tt(hs("V", 8, 16), hs("cv", 8, 16), A("kv"), AL.mult)
-        DN = {far: c("P0", 0, 128), near: c("P5", 256, 384)}
-        for h in (far, near):
-            mm(DN[h], A("ID"), pn("S1", h), True, False)
-        for h in range(2):
-            mm(c("P%d" % (1 + h), 0, 256), A("ID"), A("S2", S_[:, t, h, :]), True, False)
-        ts(A("ek"), st(t, 0), 0.5, AL.add)
-        tt(A("nf"), A("ek"), A("K"), AL.not_equal)
-        act(c("EQ", 0, n), c("EA", 0, n), AF.Relu, 1.0, -1.0)
-        if not last:
-            rep_seed(t + 1)
-        act(A("uh"), A("nf"), AF.Identity, 0.5, 64.0)
-        act(A("gk"), A("nf"), AF.Identity, 2.0, -1.0)
-        if t:
-            act(A("aj"), c("P4", 64, 80), AF.Identity, 0.0, -1.0, A("nx"))
-            act(A("r1"), A("nx"), AF.Identity, -0.46875, 1.0 / 16)
-            act(A("r2"), A("r1"), AF.Identity, BIG)
-            act(A("r3"), A("r2"), AF.Identity, -BIG)
-            act(A("a15"), A("r3"), AF.Identity, A("nx"), -16.0)
-            act(A("LI"), A("THR"), AF.Identity, A("a15"))
+        def diff_n(h):
+            mms([(pf(DN[h], 0, 0, 128), "NI", lst(t, QP, QP1, h)), (pf(DN[h], 0, 128, 144), "N16", lst(t, QK, QN + 1, h))], True)
+            act(A("AN", S_[:, h]), pf(DN[h], 0, 0, 144), AF.Abs)
+
+        def own_points(h):
+            mms([(pf(DV[h], 0, 0, 256), "ID", st(t, QP1, QEND, 1, h)), (pf(DV[h], 1, 0, 128), "ID", st(t, QP2, QEND, 1, h)),
+                 (pf(DV[h], 1, 128, 256), "ID", st(t, QP1, QP2, 1, h))])
+
+        def diff_points(h):
+            mms([(pf(DV[h], k, 0, 256), "NI", lst(t, QP1, QEND, h)) for k in range(2)], True)
+            act(c("AR", 512 * h, 512 * h + 512), A("P%d" % DV[h]), AF.Abs)
+
+        def decide(h):
+            o = ps(5, 0, None, 1, h)
+            mms([(o, "ID", c("K2K", 0, 8)), (o, "NS", q3("LI", 0, None, h)), (o, "I4", A("AN", S_[:, h, 128:144:2])),
+                 (o, "I4", A("AN", S_[:, h, 129:144:2]))]
+                + [(o, c("SEL", 15 - p, 143 - p), A("AN", S_[:, h, p:128:16])) for p in range(16)]
+                + [(o, "ID", A("K35")), (o, "NI", A("K35")), (o, "ID", c("CF", 8 * h, 8 * h + 8))], True)
+
+        def write(h):
+            tt(X(A("X"), c("SO", 8 * h, 8 * h + 8)), c("VAL", 128 * h, 128 * h + 128), A("C192"), AL.add)
+            if last and h == near:
+                dma("y", A("yx"), XT)
+
+        def new_place():
+            mms([(ps(5, 1), "ID", A("K2K")), (ps(5, 1), "ID", A("CN16")), (ps(5, 1), "N2K", OK)], True)
+            cp(A("GO"), ps(5, 1))
+
+        def weighted():
+            mms([(ps(4, 16), c("WM", 15 - p, 143 - p), A("S1", S_[:, t, :, 8 * QP + p:8 * QP1:16])) for p in range(16)], True)
+
+        def new_bias():
+            sd = c("SD", 16 * t + 16, 16 * t + 32)
+            mms([(ps(3, 0), "I16", sd), (ps(3, 0), "I16", sd), (ps(3, 0), "I1184", st(t, QN))], True)
+            act(A("y0"), ps(3, 0), AF.Copy)
+
+        todo = {"v": [(j, None) for j in range(NV[t])],
+                "s": [(j, None) for j in range(NV[t], J - ND[t])] + [(None, None)] * min(t, 1)
+                + [(j, h) for h in (far, near) for j in range(J - ND[t], J)]}
+
+        def rest(q):
+            while todo[q]:
+                gather(q, t, *todo[q].pop(0))
+
+        always = {
+            "v": lambda: gather("v", t, *todo["v"].pop(0)), "s": lambda: gather("s", t, *todo["s"].pop(0)),
+            "V": lambda: rest("v"), "S": lambda: rest("s"),
+            "scanF": lambda: scan(far), "scanN": lambda: scan(near),
+            "nF": lambda: pick(0, far), "nN": lambda: pick(0, near), "1F": lambda: pick(1, far), "1N": lambda: pick(1, near),
+            "2F": lambda: pick(2, far), "2N": lambda: pick(2, near),
+            "a": lambda: send("a", t), "b": lambda: send("b", t), "c": lambda: send("c", t), "e": lambda: send("e", t),
+            "ownF": lambda: own_n(far), "ownN": lambda: own_n(near), "ptsF": lambda: own_points(far), "ptsN": lambda: own_points(near),
+            "u": weighted,
+            "VAL": lambda: act(A("VAL"), st(t, QP, QP1), AF.Identity, 191.53125, 1.0 / 16),
+            "ui": lambda: cp(A("ui"), ps(4, 16)), "uu": lambda: ts(A("uu"), A("ui"), 4095, AL.bitwise_and),
+            "u7": lambda: ts(A("u7"), A("ui"), 7, AL.bitwise_and), "w2": lambda: ts(A("w2"), A("uu"), 1184.0, AL.add),
+            "CF": lambda: tt(A("CF"), A("u7"), A("BC"), AL.add), "pr": lambda: tt(A("pr"), A("uu"), A("w2"), AL.mult),
+            "nw": lambda: ts(A("nw"), A("pr"), 5, AL.logical_shift_right, W - 1, AL.bitwise_and),
+            "NEW": lambda: cp(A("NEW"), A("nw")),
+            "dnF": lambda: diff_n(far), "dnN": lambda: diff_n(near), "dpF": lambda: diff_points(far), "dpN": lambda: diff_points(near),
+            "decF": lambda: decide(far), "decN": lambda: decide(near),
+            "soF": lambda: cp(c("SO", 8 * far, 8 * far + 8), ps(5, 0, None, 1, far)),
+            "soN": lambda: cp(c("SO", 8 * near, 8 * near + 8), ps(5, 0, None, 1, near)),
+            "wrF": lambda: write(far), "wrN": lambda: write(near), "ok": lambda: ts(OK, ps(5, 0), float(W), AL.is_lt),
+            "e2": lambda: early2(t), "e3": lambda: early3(t), "eok": lambda: appended(t),
+            "len0": lambda: lengths(t, True), "len": lambda: lengths(t, False),
+            "EV": lambda: act(A("EV"), ps(4, 8, 12), AF.Abs), "sums": lambda: sums(t),
+        }
+        later = {
+            "L4": lambda: layer4(t), "OU": lambda: places(t),
+            "AG": lambda: ts(A("AG"), ps(4, 0, 4), 0.0, AL.is_lt), "L2": lambda: layer2(t - 1), "L3": lambda: layer3(t - 1),
+            "A": lambda: act(A("aj"), st(t, QKEEP), AF.Identity, 0.0, 1.0, A("nx")), "LI": limits,
+            "EA": lambda: slot(m, st(t, QNN)), "bnd": lambda: bounds(m),
+            "min": lambda: tt(c("TS", 0, m), pf(6, 1, 0, m), c("TS", 0, m), AL.min),
+            "max": lambda: tt(c("TS", 0, m), pf(6, 0, 0, m), c("TS", 0, m), AL.max),
+        }
+        if last:
+            ahead = {"T0": lambda: ts(A("T0"), A("TS"), -32.0, AL.add), "Z0": lambda: last_slot(0), "Z1": lambda: last_slot(1),
+                     "Z2": lambda: last_slot(2)}
         else:
-            for k in range(1, 5):
-                act(hs("THR", 8 * k, 8 * k + 8), hs("THR", 0, 8), AF.Copy)
-        lim = "LI" if t else "THR"
-        act(A("VAL"), PN, AF.Identity, 191.53125, 1.0 / 16)
-        if not last:
-            act(A("OB"), A("IL"), AF.Identity, -0.25, float(L + 1))
-        cp(A("ui"), c("P3", 16, 32))
-        ts(A("uu"), A("ui"), 4095, AL.bitwise_and)
-        ts(A("u7"), A("ui"), 7, AL.bitwise_and)
-        ts(A("w1"), A("uu"), -2048.0, AL.add)
-        ts(A("w2"), A("uu"), 3232.0, AL.add)
-        tt(A("pr"), A("w1"), A("w2"), AL.mult)
-        ts(A("c1"), A("u7"), 1.0 / W, AL.mult)
-        ts(A("nw"), A("pr"), 5, AL.arith_shift_right, W - 1, AL.bitwise_and)
-        cp(c("NEW", 0, 16), A("nw"))
-        cp(c("NEW", 16, 32), A("nw"))
-        for j in range(0, n, 32):
-            mm(c("P6", j, min(j + 32, n)), A("IH"), c("NEW", 0, min(32, n - j)), False, j + 32 >= n)
-        tt(A("CF"), A("c1"), A("BC"), AL.add)
-        tt(hs("E", 0, 32), st(t, 0, 4), lst(t, 0, 4), AL.is_equal)
-        tt(hs("E", 32, 40), st(t, 2), lst(t, 3), AL.is_equal)
-        tt(hs("E", 40, 48), st(t, 3), lst(t, 2), AL.is_equal)
-        tt(c("DL", 0, n), c("P6", 0, n), c("EQ", 0, n), AL.mult)
-        if not last:
-            mm(c("P7", 0, n), A("IH"), c("DL", 0, n), False, True)
-        tt(hs("E", 8, 16), hs("E", 0, 8), hs("E", 8, 16), AL.mult)
-        tt(A("HK"), A("uh"), A("K"), AL.mult)
-        tt(A("LM"), hs("E", 8, 48), A(lim), AL.mult)
-        tt(A("K2"), A("gk"), A("K"), AL.mult)
-        if not last:
-            hash_tail(c("P7", 0, n), t + 1)
-        mm(DN[far], A("NI"), pn("L1", far), False, True)
-        act(c("AN", 128 * far, 128 * far + 128), DN[far], AF.Abs)
-        if t:
-            mm(c("P6", 256, 256 + m), A("IF"), c("TT", 0, m), True, False)
-            mm(c("P6", 256, 256 + m), A("IH"), c("DK", 0, m), False, True)
+            hh = hashed(t + 1)
+            ahead = {"seeds": lambda: seeds(t + 1), "h0": hh[0], "h1": hh[1], "h2": hh[2], "h3": hh[3], "be": new_bias,
+                     "y1": lambda: tt(A("y1"), A("nw"), pf(7, 0, 0, 16), AL.mult),
+                     "yn": lambda: tt(A("yn"), A("y1"), A("y0"), AL.add),
+                     "yc": lambda: ts(A("yc"), A("yn"), 5, AL.arith_shift_right, W - 1, AL.bitwise_and),
+                     "cn": lambda: cp(A("CN16"), A("yc")), "GO": new_place, "e4n": lambda: early4(st(t, QN))}
+            if t:
+                ahead["G0"] = lambda: iota(A("G", S_[:, 0:256 * (L + 1):L + 1]), [[0, 256]], -256, 0)
+        step = {**always, **(later if t else {}), **ahead}
+        done = set()
+        for nm in ORDER:
+            if nm in step and (nm not in todo or todo[nm]):
+                step[nm]()
+                done.add(nm)
+        assert done | set(todo) == set(step)
 
-        mm(DN[near], A("NI"), pn("L1", near), False, True)
-        act(c("AN", 128 * near, 128 * near + 128), DN[near], AF.Abs)
-        if t:
-            act(c("TT", 0, m), c("P6", 256, 256 + m), AF.Copy)
-        rows(c("P3", 0, 16), "SEL", lambda p: A("AN", S_[:, p::16]))
-        tt(A("bad"), c("P3", 0, 16), hs("LM", 0, 8), AL.is_ge)
-        tt(A("ok"), c("P3", 0, 16), hs("LM", 0, 8), AL.is_lt)
-        tt(A("sy"), A("bad"), A("CF"), AL.add)
-        ts(A("SO"), A("sy"), float(W), AL.mult)
-        tt(X(A("X"), A("SO")), A("VAL"), A("C192"), AL.add)
-        if last:
-            dma("y", A("yx"), XT)
+    early4(A("N0"))
+    layer4(0)
+    weights()
+    places(0)
+    weights2()
+    thresholds()
+    for t in range(RO):
+        one_round(t)
 
-        for h in range(2):
-            P = "P%d" % (1 + h)
-            mm(c(P, 0, 256), A("NI"), A("L2", S_[:, t, h, :]), False, True)
-            mm(c(P, 256, 512), A("ID"), A("S2", S_[:, t, h, :]), True, False)
-            mm(c(P, 256, 384), A("NI"), A("L2", S_[:, t, h, 128:256]), False, False)
-            mm(c(P, 384, 512), A("NI"), A("L2", S_[:, t, h, 0:128]), False, True)
-            act(c("AR", 512 * h, 512 * h + 512), A(P), AF.Abs)
-        for j in range(L):
-            mm(c("P5", 16 * j, 16 * j + 16), A("ID"), A("ok"), True, True)
-        rows(c("P4", 0, 64), "SEL", lambda p: A("AR", S_[:, p::16]))
-        if not last:
-            for j in range(NE[t + 1]):
-                gather("v", t + 1, j, None)
-        else:
-            tt(c("DK", 0, n), c("DL", 0, n), c("P5", 0, n), AL.mult)
-            mm(c("P6", 256, 256 + n), A("IF"), c("TT", 0, n), True, False)
-            mm(c("P6", 256, 256 + n), A("IH"), c("DK", 0, n), False, True)
-            act(A("YT"), c("P6", 256, 256 + n), AF.Identity, -32.0)
-            dma("y", A("yt"), A("YT"))
-            tt(A("kv"), A("bad"), A("nf"), AL.mult)
-        tt(A("wn"), st(t, 1), A("ok"), AL.add)
-        tt(A("AG"), c("P4", 0, 64), hs("LM", 8, 40), AL.is_lt)
-        tt(A("av"), hs("AG", 0, 16), hs("AG", 16, 32), AL.max)
-        tt(A("cv"), A("V"), A("av"), AL.add)
-        tt(A("PT", S_[:, :, 0, :]), hs("cv", 0, 8), A("HK"), AL.is_ge)
-        tt(A("PT", S_[:, :, 1, :]), hs("cv", 8, 16), A("HK"), AL.is_ge)
-        if last:
-            tt(c("YS", 32, 48), hs("cv", 0, 8), A("kv"), AL.mult)
-        tt(A("PT", S_[:, :, 2:4, :]), A("PT", S_[:, :, 0:2, :]), st(t, 2, 4), AL.mult)
-        if last:
-            tt(c("YS", 48, 64), hs("cv", 8, 16), A("kv"), AL.mult)
-        tt(A("RQ"), A("PT", S_[:, :, 0::2, :]), A("PT", S_[:, :, 1::2, :]), AL.max)
-        rw, qq = A("RQ", S_[:, :, 0, :]), A("RQ", S_[:, :, 1, :])
-        tt(A("keep"), rw, A("ok"), AL.is_le)
-        tt(A("nor"), A("bad"), rw, AL.is_gt)
-        tt(A("xn"), A("keep"), A("wn"), AL.mult)
-        if last:
-            tt(A("t0"), A("nor"), A("ek"), AL.mult)
-            tt(A("zz"), qq, A("xn"), AL.max)
-            ts(c("YS", 16, 32), A("t0"), 0.5, AL.max, 2.0, AL.mult)
-            ts(c("YS", 0, 16), A("zz"), -0.25, AL.add)
-            dma("s", A("yst"), A("YS"))
-        else:
-            tt(A("t1"), A("nor"), A("K2"), AL.mult)
-            tt(st(t + 1, 1), qq, A("xn"), AL.max)
-            rounders("t1")
-            ts(A("K"), A("t1"), 1.0, AL.max)
-            tt(A("t0"), A("nor"), A("ek"), AL.mult)
-            mm(c("P4", 64, 80), A("ON"), A("keep"), True, True)
-            points_of(t + 1)
-            ts(st(t + 1, 0), A("t0"), 0.5, AL.max)
+    t = RO - 1
+    n = 16 * SLOTS
+    ts(A("AG"), ps(4, 0, 4), 0.0, AL.is_lt)
+    layer2(t)
+    mms([(pf(2, 1, 0, n), "ID", A("EA")), (pf(2, 0, 0, n), "NI", A("EA"))], True)
+    tt(A("T0"), pf(2, 1, 0, n), A("T0"), AL.min)
+    layer3(t)
+    tt(A("YT"), pf(2, 0, 0, n), A("T0"), AL.max)
+    mms([(ps(1, 0), "NI", st(RO, QT1)), (ps(1, 0), "NI", st(RO, QT2)), (ps(1, 1), "ID", st(RO, QK)),
+         (ps(1, 2, 4), "ID", st(RO, QV1, QV2 + 1, 2))], True)
+    for h in range(2):
+        act(A("YS", S_[:, :, h, :]), ps(1, 0, 4, 1, h), AF.Copy)
+    dma("y", A("yt"), A("YT"))
+    dma("s", A("yst"), A("YS"))
 
     for sem, val in cnt.items():
         wait("g", sem, val)

@@ -17,7 +17,7 @@ def _sb(n, d):
 
 
 SCRATCH = {
-    "X": _sb(3 * W, B), "G": _sb(256 * 13, B), "R": _sb(256 * 13, B), "GN": _sb(256, B),
+    "X": _sb(3 * W, B), "G": _sb(256 * 13, B), "R": _sb(256 * 13, B), "MK": _sb(128 * 13, B), "X2": _sb(2 * W + W // 2, B),
     "y0": _sb(16, F), "y1": _sb(16, F), "yn": _sb(16, I), "yc": _sb(16, I), "CN16": _sb(16, H), "GO": _sb(16, U), "T0": _sb(224, F),
     "S1": _sb([RO + 1, 2, 8 * QEND], B), "L1": _sb([RO, 2, 8 * QEND], B),
     "tri": _sb(224, I), "sdi": _sb(80, I), "n0i": _sb(16, I), "k0i": _sb(16, I), "thi": _sb(16, I), "wti": _sb(1, I),
@@ -27,26 +27,33 @@ SCRATCH = {
     "pi": _sb(1, I), "pa": _sb(1, I), "pb": _sb(1, I), "pf": _sb(1, F), "gf": _sb(1, F), "pm": _sb(1, F),
     "wa": _sb(1, I), "wb": _sb(1, I), "wf": _sb(1, F), "K2K": _sb(16, B), "K35": _sb(8, B), "K27": _sb(1, B), "K75": _sb(1, B),
     "IA": _sb(16, F), "IB": _sb(48, F), "IL": _sb(48, F), "BC": _sb(16, F), "OB": _sb([RO, 48], H), "OU": _sb(48, U),
-    "TH": _sb([2, 4, 8], F), "LI": _sb([2, 4, 8], H), "EV": _sb([2, 4, 8], B), "AG": _sb([2, 4, 8], B), "BB": _sb([2, 2, 8], B),
-    "AN": _sb([2, 144], B), "AR": _sb(1024, B), "VAL": _sb(256, B), "C192": _sb(128, B),
+    "TH": _sb([2, 4, 8], F), "LI": _sb([2, 4, 8], H), "EV": _sb([2, 48], B), "AG": _sb([2, 4, 8], B), "BB": _sb([2, 2, 8], B),
+    "AN": _sb([2, 128], B), "AR": _sb(1024, B), "VAL": _sb(256, B), "C192": _sb(128, B),
     "ui": _sb(16, I), "uu": _sb(16, I), "u7": _sb(16, I), "w2": _sb(16, F), "pr": _sb(16, I), "nw": _sb(16, I),
     "NEW": _sb(16, H), "CF": _sb(16, H), "SO": _sb(16, U), "ok": _sb(16, B), "N0": _sb(16, B),
     "b2": _sb(16, F), "b4": _sb(16, F), "b8": _sb(16, F), "t0": _sb(16, F), "aj": _sb(16, F), "nx": _sb(1, F),
-    "YS": _sb([4, 2, 8], F), "YT": _sb(224, F),
+    "YS": _sb(64, F), "YT": _sb(224, F),
 }
 for _n in SCALES:
     SCRATCH[_n] = _sb(128, B)
 for _i in range(8):
     SCRATCH["P%d" % _i] = ("psum", [128, 2, 32, 8], F)
 
-SEMAPHORES = (["cv_", "cs_", "ct_", "cg_", "loc"] + ["d%d" % i for i in range(10)]
-              + ["%s%d" % (n, t) for t in range(RO) for n in "abce"])
+SEMAPHORES = (["cv_", "cs_", "ct_", "cg_", "loc"] + ["d%d" % i for i in range(11)]
+              + ["%s%d" % (n, t) for t in range(RO) for n in "abcek"])
 
 NV = [4, 3, 4, 4, 4]
 ND = [3, 3, 3, 4, 4]
-ORDER = """s s s v AG s s s s v s L2 v L3 v L4 s be scanF s OU S V nF a A scanN nN b seeds EA bnd 1F 2F c 2N 1N e G0
-    LI u min ownF ui uu ptsF ptsN len0 u7 ownN max w2 pr dnF h0 CF h1 nw Z0 T0 decF y1 NEW dnN yn h2 VAL len yc EV soF
-    dpF h3 decN cn wrF soN ok dpN e4n wrN e2 e3 Z2 GO sums Z1 eok""".split()
+ORDER = [x.split() for x in (
+    """s K1 K2 s v K3 s K5 s s s v be v W1 v W2 s K4 len0 s scanF W3 nF scanN 1F W4 nN seeds a ownF u h0 2F 2N b c ui 1N VAL len TH
+    ownN h1 uu u7 EV V ptsN ptsF h2 dnF S e w2 CF XZ pr h3 dnN nw decF y1 soF decN yn wrF soN yc dpN NEW ok e4n dpF e2 cn wrN GO
+    e3 sums eok""",
+    """s v s AG v L2 v s L3 s s s s s s v s L4 scanF S OU nF scanN A len0 EA seeds ownF be nN bnd 2F 2N min LI u ui max uu ownN 1N
+    1F VAL h0 k a w2 u7 len ptsN EV dnF pr b ptsF CF h1 nw c dnN y1 h2 e NEW yn decF soF h3 decN dpF wrF V soN yc wrN e2 dpN G0
+    cn ok e3 e4n GO sums eok""",
+    """s v s s AG s s v L2 v s L3 v s L4 s s OU scanF s S scanN nF e2 len0 nN EA 1F A 1N k ownF 2F bnd a min len b EV 2N VAL c u max
+    ui X2 ownN LI u7 ptsF Z0 dnF ptsN dnN CF uu e decF decN w2 dpF V pr e3 dpN T0 nw soF NEW wrF soN ok Z1 Z2 sums Z3 wrN eok AGz
+    Z4 L2z yt L3z yst""")]
 AL = AluOpType
 AF = ActivationFunctionType
 S_ = np.s_
@@ -118,7 +125,7 @@ def rank_program(g, core, T, topo):
                 for arr in [lw[a[0]]] + list(lr[a[0]].values()):
                     for p in np.unique(arr[e]):
                         if p:
-                            add(int(p), False)
+                            add(int(p), q != "t")
         for a in rd + wr:
             if a[0] in bank:
                 for s, p in bank[a[0]].items():
@@ -202,24 +209,25 @@ def rank_program(g, core, T, topo):
     eng = [list(topo.engines(core, m)) for m in mate]
     far = 0 if len(eng[0]) < len(eng[1]) else 1
     near = 1 - far
-    eng[near] = [e for e in eng[near] if e not in eng[far]]
-    msk = [sum(1 << e for e in es) for es in eng]
+    left = [e for e in eng[near] if e not in eng[far]]
     dst = []
     for m in mate:
         rid, pid = topo.addr(m, core)
         dst.append(DstId(rid=rid, pnc=pid))
-    MSG = {"a": (far, QK, QP1), "b": (near, QK, QP1), "c": (far, QP1, QEND), "e": (near, QP1, QEND)}
+    MSG = {"k": (QK, QP, {far: eng[far], near: left}), "a": (QP, QP1, {far: eng[far]}), "b": (QP, QP1, {near: eng[near]}),
+           "c": (QP1, QEND, {far: eng[far]}), "e": (QP1, QEND, {near: left})}
     for t in range(RO):
-        for nm, (h, a, b) in MSG.items():
-            mark(A("L1", S_[:, t, h, 8 * a:8 * b]), "%s%d" % (nm, t), len(eng[h]))
+        for nm, (a, b, es) in MSG.items():
+            for h in es:
+                mark(A("L1", S_[:, t, h, 8 * a:8 * b]), "%s%d" % (nm, t), sum(len(e) for e in es.values()))
 
     def send(nm, t):
-        h, a, b = MSG[nm]
-        cnt["loc"] = cnt.get("loc", 0) + len(eng[h])
-        order("g", [A("S1", S_[:, t, h, 8 * a:8 * b])], [], "loc", cnt["loc"])
-        g.remote_dma_fused([RemoteDMATransfer(dst_ids=[dst[h]], dma_engine_mask=msk[h], remote_sem=T.sem["%s%d" % (nm, t)],
-                                              src=T["S1"][:, t, h, 8 * a:8 * b], dst=T["L1"][:, t, h, 8 * a:8 * b])],
-                           local_sem=T.sem["loc"])
+        a, b, es = MSG[nm]
+        cnt["loc"] = cnt.get("loc", 0) + sum(len(e) for e in es.values())
+        order("g", [A("S1", S_[:, t, h, 8 * a:8 * b]) for h in es], [], "loc", cnt["loc"])
+        g.remote_dma_fused([RemoteDMATransfer(dst_ids=[dst[h]], dma_engine_mask=sum(1 << e for e in es[h]),
+                                              remote_sem=T.sem["%s%d" % (nm, t)], src=T["S1"][:, t, h, 8 * a:8 * b],
+                                              dst=T["L1"][:, t, h, 8 * a:8 * b]) for h in es], local_sem=T.sem["loc"])
 
     def sl(a, b, s):
         return a if b is None else slice(a, b, s)
@@ -250,20 +258,21 @@ def rank_program(g, core, T, topo):
     ON16, OK = c("ON", 0, 16), A("ok")
     DN = {far: 0, near: 1}
     DV = {far: 2, near: 3}
+    DS = {far: 4, near: 5}
 
     dma("y", A("tri"), A("tr"))
     dma("s", A("sdi"), A("sd"))
     dma("s", A("k0i"), A("k0"))
     dma("y", A("n0i"), A("n0"))
-    dma("s", A("wti"), A("wt"))
-    dma("y", A("thi"), A("th"))
     dma("y", XT, A("xt"))
+    dma("y", A("wti"), A("wt"))
+    dma("y", A("thi"), A("th"))
     iota(A("pi"), [[0, 1]], 0, 1)
     iota(A("IC"), [[1, 144]], 0, 0)
     iota(A("BE"), [[1184, SLOTS], [0, 16]], -1024, 0)
     iota(A("IB"), [[0, 6], [16, 8]], 0, 0)
     iota(A("IA"), [[16, 16]], 0, 0)
-    iota(A("G", S_[:, 0:256 * (TOP + 1):TOP + 1]), [[0, 256]], -256, 0)
+    iota(A("G", S_[:, 0:256 * (TOP + 1):TOP + 1]), [[0, 256]], 0, 0)
     iota(A("JC"), [[1, SLOTS], [0, 16]], 0, 0)
     fill(A("C2080"), 2080.0)
     fill(A("ON"), 1.0)
@@ -274,7 +283,8 @@ def rank_program(g, core, T, topo):
     ts(A("ID"), c("IC", 0, 128), A("pf"), AL.is_equal)
     cp(A("pm"), A("pa"))
     ts(A("gf"), A("pb"), 15.0, AL.add)
-    fill(c("X", W, 2 * W), 0.0)
+    fill(A("MK"), 1.0)
+    iota(A("MK", S_[:, 0:128 * (TOP + 1):TOP + 1]), [[0, 128]], 0, 0)
     for nm in list(SCALES)[1:]:
         act(A(nm), A("ID"), AF.Identity, 0.0, SCALES[nm])
     ts(A("IL"), A("IB"), A("pm"), AL.add)
@@ -295,38 +305,37 @@ def rank_program(g, core, T, topo):
                 lambda: ts(c("YB", 0, n), c("YI", 0, n), 5, AL.logical_shift_right, W - 1, AL.bitwise_and),
                 lambda: cp(c("CI", 0, n), c("YB", 0, n))]
 
-    h0 = hashed(0)
     ts(A("SD"), A("sdi"), -2048.0, AL.add)
     ts(A("TS"), A("tri"), 32.0, AL.add)
     seeds(0)
-    ts(A("b2"), A("k0i"), 2.0, AL.is_ge)
-    ts(A("b4"), A("k0i"), 4.0, AL.is_ge, 3.0, AL.mult)
-    h0[0]()
-    ts(A("b8"), A("k0i"), 8.0, AL.is_ge, 7.0, AL.mult)
-    tt(A("t0"), A("b2"), A("b4"), AL.max)
-    h0[1]()
-    ts(st(0, QK), A("k0i"), -1.0, AL.add)
-    tt(st(0, QKK), A("t0"), A("b8"), AL.max)
-    h0[2]()
-    cp(A("N0"), A("n0i"))
     ts(st(0, QV1, QV2 + 1, 2), c("ON", 0, 32), 0.0, AL.mult)
-    h0[3]()
+    ts(A("BC"), A("IA"), A("pm"), AL.add, 8.0, AL.mult)
+    for f in hashed(0):
+        f()
+
+    def counts():
+        ts(A("b2"), A("k0i"), 2.0, AL.is_ge)
+        ts(A("b4"), A("k0i"), 4.0, AL.is_ge, 3.0, AL.mult)
+        ts(A("b8"), A("k0i"), 8.0, AL.is_ge, 7.0, AL.mult)
+        ts(st(0, QK), A("k0i"), -1.0, AL.add)
+        cp(A("N0"), A("n0i"))
+        tt(A("t0"), A("b2"), A("b4"), AL.max)
+
+    def counts2():
+        tt(st(0, QKK), A("t0"), A("b8"), AL.max)
+        early4(A("N0"))
+
     for t in range(RO):
         act(A("OB", S_[:, t]), A("IL"), AF.Identity, 0.0, float(steps(t) + 1))
     act(A("OP"), c("ON", 0, 128), AF.Identity, 0.0, 1.0 / 16)
     act(A("OM"), c("ON", 0, 128), AF.Identity, 0.0, -1.0 / 16)
-    for nm, n, v in (("K27", 1, 1.5 * 2.0 ** 27), ("K75", 1, 7.5), ("K2K", 16, 2048.0), ("K35", 8, 1.5 * 2.0 ** 35), ("C192", 128, -192.0)):
+    for nm, n, v in (("K27", 1, 1.5 * 2.0 ** 27), ("K75", 1, 7.5), ("K2K", 16, 2048.0), ("K35", 8, 1.5 * 2.0 ** 35),
+                     ("C192", 128, -192.0)):
         act(A(nm), c("ON", 0, n), AF.Identity, 0.0, v)
 
     def weights():
         ts(A("wa"), A("wti"), 2048.0, AL.add)
         ts(q3("TH", 0), A("thi"), 0.5, AL.add)
-        ts(A("wb"), A("wa"), 4095, AL.bitwise_and)
-        ts(A("BC"), A("IA"), A("pm"), AL.add, 8.0, AL.mult)
-        ts(A("wf"), A("wb"), -2048.0, AL.add)
-
-    def weights2():
-        ts(A("WM"), A("IC"), A("gf"), AL.is_equal, A("wf"), AL.mult)
 
     def thresholds():
         for k in range(1, 4):
@@ -336,7 +345,7 @@ def rank_program(g, core, T, topo):
     def gather(q, t, j, h):
         L = steps(t) + 1
         if j is None:
-            act(A("GN"), X(c("X", 0, 2 * W), A("GO")), AF.Copy)
+            act(A("G", S_[:, 0:256 * L:L]), X(c("X", 0, 2 * W), A("GO")), AF.Copy)
             return
         if h is None:
             o, off = A("G", S_[:, 1 + j:256 * L:L]), c("CI", 16 * j, 16 * j + 16)
@@ -366,17 +375,18 @@ def rank_program(g, core, T, topo):
         if t < RO - 1:
             mms([(ps(1, 0), "N16", OK)] + [(ps(1, k), "ID", OK) for k in (1, 3, 4)])
         else:
-            mms([(ps(1, 0), "ID", st(t, QN)), (ps(1, 0), "ID", OK), (ps(1, 1), "ID", ON16)])
+            mms([(pf(1, 0, 0, 16), "ID", st(t, QN)), (pf(1, 0, 0, 16), "ID", OK), (pf(1, 0, 16, 32), "ID", ON16)])
 
     def lengths(t, own):
         q1, qK = lst(t, QM1), lst(t, QKK)
-        mms([(ps(4, 9, 12, 2), "I16", c("ON", 0, 32))] + [(ps(4, k), "I16", st(t, QM1)) for k in (8, 11)]
-            + [(ps(4, k), "I16", st(t, QM2)) for k in (9, 10)] if own else
-            [(ps(4, k), "N16", q1) for k in (8, 9, 10, 11)] + [(ps(4, k), "I16", qK) for k in (9, 11)], not own)
+        mms([(ps(2, 9, 12, 2), "I16", c("ON", 0, 32))] + [(ps(2, k), "I16", st(t, QM1)) for k in (8, 11)]
+            + [(ps(2, k), "I16", st(t, QM2)) for k in (9, 10)] + [(ps(2, 12, 14), "I16", st(t, QK, QN + 1))] if own else
+            [(ps(2, k), "N16", q1) for k in (8, 9, 10, 11)] + [(ps(2, k), "I16", qK) for k in (9, 11)]
+            + [(ps(2, 12, 14), "N16", lst(t, QK, QN + 1))], not own)
 
     def sums(t):
-        mms([(ps(4, 0, 4), "NS", A("LI"))] + [(ps(4, 0, 4), c("SEL", 15 - p, 143 - p), A("AR", S_[:, p::16])) for p in range(16)]
-            + [(ps(4, 0, 4), "I4", A("EV"))], True)
+        mms([(ps(4, 0, 4), "NS", A("LI")), (ps(4, 0, 4), "I4", A("EV", S_[:, :, 0:32]))]
+            + [(ps(4, 0, 4), c("SEL", 15 - p, 143 - p), A("AR", S_[:, p::16])) for p in range(16)], True)
 
     def counted(k, m, stop):
         mms([(ps(k, 0, 2), m, q3("AG", 0, 2)), (ps(k, 0), m, q3("AG", 3)), (ps(k, 1), m, q3("AG", 2))], stop)
@@ -428,8 +438,23 @@ def rank_program(g, core, T, topo):
         elif k == 1:
             mms([(pf(6, 0, j, j + 16), "N16", OK) for j in every], True)
             act(A("EA"), pf(6, 0, 0, n), AF.Abs, 0.0, 4096.0)
-        else:
+        elif k == 2:
             mms([(pf(2, 0, j, j + 16), "ID", A("NEW")) for j in every])
+        else:
+            mms([(pf(2, 1, 0, n), "ID", A("EA")), (pf(2, 0, 0, n), "NI", A("EA"))], True)
+
+    def transcripts():
+        tt(A("YT"), pf(2, 0, 0, 16 * SLOTS), A("T0"), AL.max)
+        dma("y", A("yt"), A("YT"))
+
+    def lanes():
+        mms([(pf(1, 0, 16 * k, 16 * k + 16), m, st(RO, q))
+             for k, m, q in ((1, "ID", QK), (2, "ID", QV1), (3, "ID", QV2), (0, "NI", QT1), (0, "NI", QT2))], True)
+        act(A("YS"), pf(1, 0, 0, 64), AF.Copy)
+        dma("s", A("yst"), A("YS"))
+
+    def agreed():
+        ts(A("AG"), ps(4, 0, 4), 0.0, AL.is_lt)
 
     def one_round(t):
         J = steps(t)
@@ -441,24 +466,28 @@ def rank_program(g, core, T, topo):
             return c(nm, 128 * L * h, 128 * L * (h + 1))
 
         def scan(h):
-            o, d0, d1 = win("R", h), win("G", h), c("X", W, W + 128 * L)
-            emit("v", lambda: g.vector.tensor_tensor_scan(ap(o), ap(d0), ap(d1), 0.0, AL.add, AL.max), [o], [d0, d1])
+            o, d0, d1 = win("R", h), c("MK", 0, 128 * L), win("G", h)
+            emit("v", lambda: g.vector.tensor_tensor_scan(ap(o), ap(d0), ap(d1), 0.0, AL.mult, AL.add), [o], [d0, d1])
 
-        def pick(k, h):
+        def pick(k, h, q):
             o, src = st(t, QP + 16 * k, QP + 16 * k + 16, 1, h), X(win("R", h), c("OU", 24 * h + 8 * k, 24 * h + 8 * k + 8))
             if k == 2:
-                act(o, src, AF.Copy)
-            elif t:
-                tt(o, src, c("GN", 128 * h, 128 * h + 128), AL.add)
-            else:
+                tt(o, src, A("G", S_[:, 128 * L * h:128 * L * (h + 1):L]), AL.subtract)
+            elif q == "v":
                 cp(o, src)
+            else:
+                act(o, src, AF.Copy)
 
         def own_n(h):
-            mms([(pf(DN[h], 0, 0, 128), "ID", st(t, QP, QP1, 1, h)), (pf(DN[h], 0, 128, 144), "I16", st(t, QK, QN + 1, 1, h))])
+            mm(pf(DN[h], 0, 0, 128), "ID", st(t, QP, QP1, 1, h))
 
         def diff_n(h):
-            mms([(pf(DN[h], 0, 0, 128), "NI", lst(t, QP, QP1, h)), (pf(DN[h], 0, 128, 144), "N16", lst(t, QK, QN + 1, h))], True)
-            act(A("AN", S_[:, h]), pf(DN[h], 0, 0, 144), AF.Abs)
+            mm(pf(DN[h], 0, 0, 128), "NI", lst(t, QP, QP1, h), True)
+            act(A("AN", S_[:, h]), pf(DN[h], 0, 0, 128), AF.Abs)
+
+        def marks():
+            iota(A("MK", S_[:, 0:128 * L:L]), [[0, 128]], 1, 0)
+            iota(A("MK", S_[:, 0:128 * (L + 1):L + 1]), [[0, 128]], 0, 0)
 
         def own_points(h):
             mms([(pf(DV[h], 0, 0, 256), "ID", st(t, QP1, QEND, 1, h)), (pf(DV[h], 1, 0, 128), "ID", st(t, QP2, QEND, 1, h)),
@@ -469,16 +498,19 @@ def rank_program(g, core, T, topo):
             act(c("AR", 512 * h, 512 * h + 512), A("P%d" % DV[h]), AF.Abs)
 
         def decide(h):
-            o = ps(5, 0, None, 1, h)
-            mms([(o, "ID", c("K2K", 0, 8)), (o, "NS", q3("LI", 0, None, h)), (o, "I4", A("AN", S_[:, h, 128:144:2])),
-                 (o, "I4", A("AN", S_[:, h, 129:144:2]))]
+            o = ps(DS[h], 0, None, 1, h)
+            mms([(o, "ID", c("K2K", 0, 8)), (o, "NS", q3("LI", 0, None, h)), (o, "I4", A("EV", S_[:, h, 32:48:2])),
+                 (o, "I4", A("EV", S_[:, h, 33:48:2]))]
                 + [(o, c("SEL", 15 - p, 143 - p), A("AN", S_[:, h, p:128:16])) for p in range(16)]
-                + [(o, "ID", A("K35")), (o, "NI", A("K35")), (o, "ID", c("CF", 8 * h, 8 * h + 8))], True)
+                + [(o, "ID", A("K35")), (o, "NI", A("K35"))] + [(o, "NH", c("K2K", 0, 8))] * (h if last and h == near else 0)
+                + [(o, "ID", c("CF", 8 * h, 8 * h + 8))], True)
 
         def write(h):
-            tt(X(A("X"), c("SO", 8 * h, 8 * h + 8)), c("VAL", 128 * h, 128 * h + 128), A("C192"), AL.add)
-            if last and h == near:
-                dma("y", A("yx"), XT)
+            to = "X2" if last and h == near else "X"
+            tt(X(A(to), c("SO", 8 * h, 8 * h + 8)), c("VAL", 128 * h, 128 * h + 128), A("C192"), AL.add)
+            if last:
+                a = W // 2 * h
+                dma("y", c("yx", a, a + W // 2), c(to, 0, W // 2) if h == near else c(to, a, a + W // 2))
 
         def new_place():
             mms([(ps(5, 1), "ID", A("K2K")), (ps(5, 1), "ID", A("CN16")), (ps(5, 1), "N2K", OK)], True)
@@ -504,8 +536,8 @@ def rank_program(g, core, T, topo):
             "v": lambda: gather("v", t, *todo["v"].pop(0)), "s": lambda: gather("s", t, *todo["s"].pop(0)),
             "V": lambda: rest("v"), "S": lambda: rest("s"),
             "scanF": lambda: scan(far), "scanN": lambda: scan(near),
-            "nF": lambda: pick(0, far), "nN": lambda: pick(0, near), "1F": lambda: pick(1, far), "1N": lambda: pick(1, near),
-            "2F": lambda: pick(2, far), "2N": lambda: pick(2, near),
+            "nF": lambda: pick(0, far, "s"), "nN": lambda: pick(0, near, "v"), "1F": lambda: pick(1, far, "s"),
+            "1N": lambda: pick(1, near, "s"), "2F": lambda: pick(2, far, "v"), "2N": lambda: pick(2, near, "v"),
             "a": lambda: send("a", t), "b": lambda: send("b", t), "c": lambda: send("c", t), "e": lambda: send("e", t),
             "ownF": lambda: own_n(far), "ownN": lambda: own_n(near), "ptsF": lambda: own_points(far), "ptsN": lambda: own_points(near),
             "u": weighted,
@@ -517,16 +549,21 @@ def rank_program(g, core, T, topo):
             "NEW": lambda: cp(A("NEW"), A("nw")),
             "dnF": lambda: diff_n(far), "dnN": lambda: diff_n(near), "dpF": lambda: diff_points(far), "dpN": lambda: diff_points(near),
             "decF": lambda: decide(far), "decN": lambda: decide(near),
-            "soF": lambda: cp(c("SO", 8 * far, 8 * far + 8), ps(5, 0, None, 1, far)),
-            "soN": lambda: cp(c("SO", 8 * near, 8 * near + 8), ps(5, 0, None, 1, near)),
-            "wrF": lambda: write(far), "wrN": lambda: write(near), "ok": lambda: ts(OK, ps(5, 0), float(W), AL.is_lt),
+            "soF": lambda: cp(c("SO", 8 * far, 8 * far + 8), ps(DS[far], 0, None, 1, far)),
+            "soN": lambda: cp(c("SO", 8 * near, 8 * near + 8), ps(DS[near], 0, None, 1, near)),
+            "wrF": lambda: write(far), "wrN": lambda: write(near), "ok": lambda: ts(OK, A("SO"), float(W), AL.is_lt),
             "e2": lambda: early2(t), "e3": lambda: early3(t), "eok": lambda: appended(t),
             "len0": lambda: lengths(t, True), "len": lambda: lengths(t, False),
-            "EV": lambda: act(A("EV"), ps(4, 8, 12), AF.Abs), "sums": lambda: sums(t),
+            "EV": lambda: act(A("EV"), ps(2, 8, 14), AF.Abs), "sums": lambda: sums(t),
         }
+        first = {"K1": counts, "K2": counts2, "K3": lambda: layer4(0), "K4": lambda: places(0), "K5": lambda: send("k", 0),
+                 "W1": weights, "W2": lambda: ts(A("wb"), A("wa"), 4095, AL.bitwise_and),
+                 "W3": lambda: ts(A("wf"), A("wb"), -2048.0, AL.add),
+                 "W4": lambda: ts(A("WM"), A("IC"), A("gf"), AL.is_equal, A("wf"), AL.mult),
+                 "TH": thresholds, "XZ": lambda: fill(c("X", W, 2 * W), 0.0)}
         later = {
-            "L4": lambda: layer4(t), "OU": lambda: places(t),
-            "AG": lambda: ts(A("AG"), ps(4, 0, 4), 0.0, AL.is_lt), "L2": lambda: layer2(t - 1), "L3": lambda: layer3(t - 1),
+            "k": lambda: send("k", t), "L4": lambda: layer4(t), "OU": lambda: places(t),
+            "AG": agreed, "L2": lambda: layer2(t - 1), "L3": lambda: layer3(t - 1),
             "A": lambda: act(A("aj"), st(t, QKEEP), AF.Identity, 0.0, 1.0, A("nx")), "LI": limits,
             "EA": lambda: slot(m, st(t, QNN)), "bnd": lambda: bounds(m),
             "min": lambda: tt(c("TS", 0, m), pf(6, 1, 0, m), c("TS", 0, m), AL.min),
@@ -534,7 +571,10 @@ def rank_program(g, core, T, topo):
         }
         if last:
             ahead = {"T0": lambda: ts(A("T0"), A("TS"), -32.0, AL.add), "Z0": lambda: last_slot(0), "Z1": lambda: last_slot(1),
-                     "Z2": lambda: last_slot(2)}
+                     "Z2": lambda: last_slot(2), "Z3": lambda: last_slot(3),
+                     "Z4": lambda: tt(A("T0"), pf(2, 1, 0, 16 * SLOTS), A("T0"), AL.min), "yt": transcripts,
+                     "AGz": agreed, "L2z": lambda: layer2(t), "L3z": lambda: layer3(t), "yst": lanes,
+                     "X2": lambda: act(c("X2", 0, W // 2), c("X", W // 2 * near, W // 2 * (near + 1)), AF.Copy)}
         else:
             hh = hashed(t + 1)
             ahead = {"seeds": lambda: seeds(t + 1), "h0": hh[0], "h1": hh[1], "h2": hh[2], "h3": hh[3], "be": new_bias,
@@ -543,38 +583,17 @@ def rank_program(g, core, T, topo):
                      "yc": lambda: ts(A("yc"), A("yn"), 5, AL.arith_shift_right, W - 1, AL.bitwise_and),
                      "cn": lambda: cp(A("CN16"), A("yc")), "GO": new_place, "e4n": lambda: early4(st(t, QN))}
             if t:
-                ahead["G0"] = lambda: iota(A("G", S_[:, 0:256 * (L + 1):L + 1]), [[0, 256]], -256, 0)
-        step = {**always, **(later if t else {}), **ahead}
+                ahead["G0"] = marks
+        step = {**always, **(later if t else first), **ahead}
         done = set()
-        for nm in ORDER:
-            if nm in step and (nm not in todo or todo[nm]):
+        for nm in ORDER[min(t, 1) + last]:
+            if nm not in todo or todo[nm]:
                 step[nm]()
                 done.add(nm)
         assert done | set(todo) == set(step)
 
-    early4(A("N0"))
-    layer4(0)
-    weights()
-    places(0)
-    weights2()
-    thresholds()
     for t in range(RO):
         one_round(t)
-
-    t = RO - 1
-    n = 16 * SLOTS
-    ts(A("AG"), ps(4, 0, 4), 0.0, AL.is_lt)
-    layer2(t)
-    mms([(pf(2, 1, 0, n), "ID", A("EA")), (pf(2, 0, 0, n), "NI", A("EA"))], True)
-    tt(A("T0"), pf(2, 1, 0, n), A("T0"), AL.min)
-    layer3(t)
-    tt(A("YT"), pf(2, 0, 0, n), A("T0"), AL.max)
-    mms([(ps(1, 0), "NI", st(RO, QT1)), (ps(1, 0), "NI", st(RO, QT2)), (ps(1, 1), "ID", st(RO, QK)),
-         (ps(1, 2, 4), "ID", st(RO, QV1, QV2 + 1, 2))], True)
-    for h in range(2):
-        act(A("YS", S_[:, :, h, :]), ps(1, 0, 4, 1, h), AF.Copy)
-    dma("y", A("yt"), A("YT"))
-    dma("s", A("yst"), A("YS"))
 
     for sem, val in cnt.items():
         wait("g", sem, val)

import numpy as np
from concourse.bass import DstId, RemoteDMATransfer
from concourse.mybir import AluOpType, ActivationFunctionType

RO, TOP, SLOTS, W = 5, 9, 14, 2048
PM = (1, 4)
F, B, I, U, H = "float32", "bfloat16", "int32", "uint16", "float16"
QV1, QV2, QT1, QT2, QKEEP, QK, QKK = 0, 2, 4, 6, 8, 10, 12
QNN, QM2, QG, QN, QM1 = 5, 7, 9, 11, 13
QP, QP1, QP2, QEND = 14, 30, 46, 62
SCALES = {"ID": 1.0, "NI": -1.0, "I16": 16.0, "NH": -0.5, "N15": -1.5, "N31": -31.0, "CP": 1.125 * 2.0 ** 24,
          "CN": -1.125 * 2.0 ** 24, "I1184": 1184.0, "N16": -16.0, "I2": 2.0, "I4": 4.0, "NS": -1.0 / 8, "N2K": -2048.0}


def _sb(n, d):
    return ("sbuf", [128] + (n if isinstance(n, list) else [n]), d)


SCRATCH = {
    "X": _sb(3 * W, B), "G": _sb(256 * 13, B), "R": _sb(256 * 13, B), "MK": _sb(128 * 13, B), "X2": _sb(2 * W + W // 2, B),
    "y0": _sb(16, F), "y1": _sb(16, F), "yn": _sb(16, I), "yc": _sb(16, I), "CN16": _sb(16, H), "GO": _sb(16, U), "T0": _sb(224, F),
    "S1": _sb([RO + 1, 2, 8 * QEND], B), "L1": _sb([RO, 2, 8 * QEND], B),
    "tri": _sb(224, I), "sdi": _sb(80, I), "n0i": _sb(16, I), "k0i": _sb(16, I), "thi": _sb(16, I), "wti": _sb(1, I),
    "TS": _sb(224, F), "SD": _sb(80, H), "EA": _sb(224, B), "C32": _sb(224, B), "C2080": _sb(224, B),
    "YI": _sb(224, I), "YB": _sb(224, I), "CI": _sb(224, U), "BE": _sb(224, F), "JC": _sb(224, B),
    "IC": _sb(144, F), "SEL": _sb(144, B), "WM": _sb(144, H), "ON": _sb(224, B), "OP": _sb(128, F), "OM": _sb(128, F),
    "pi": _sb(1, I), "pa": _sb(1, I), "pb": _sb(1, I), "pf": _sb(1, F), "gf": _sb(1, F), "pm": _sb(1, F),
    "wa": _sb(1, I), "wb": _sb(1, I), "wf": _sb(1, F), "K2K": _sb(16, B), "K35": _sb(8, B), "K27": _sb(1, B), "K75": _sb(1, B),
    "IA": _sb(16, F), "IB": _sb(48, F), "IL": _sb(48, F), "BC": _sb(16, F), "OB": _sb([RO, 48], H), "OU": _sb(48, U),
    "TH": _sb([2, 4, 8], F), "LI": _sb([2, 4, 8], H), "EV": _sb([2, 48], B), "AG": _sb([2, 4, 8], B), "BB": _sb([2, 2, 8], B),
    "AN": _sb([2, 128], B), "AR": _sb(1024, B), "VAL": _sb(256, B), "C192": _sb(128, B),
    "ui": _sb(16, I), "uu": _sb(16, I), "u7": _sb(16, I), "w2": _sb(16, F), "pr": _sb(16, I), "nw": _sb(16, I),
    "NEW": _sb(16, H), "CF": _sb(16, H), "SO": _sb(16, U), "ok": _sb(16, B), "N0": _sb(16, B),
    "b2": _sb(16, F), "b4": _sb(16, F), "b8": _sb(16, F), "t0": _sb(16, F), "aj": _sb(16, F), "nx": _sb(1, F),
    "YS": _sb(64, F), "YT": _sb(224, F),
}
for _n in SCALES:
    SCRATCH[_n] = _sb(128, B)
for _i in range(8):
    SCRATCH["P%d" % _i] = ("psum", [128, 2, 32, 8], F)

SEMAPHORES = (["cv_", "cs_", "ct_", "cg_", "loc"] + ["d%d" % i for i in range(11)]
              + ["%s%d" % (n, t) for t in range(RO) for n in "abcek"])

NV = [4, 3, 4, 4, 4]
ND = [3, 3, 3, 4, 4]
ORDER = [x.split() for x in (
    """s K1 K2 s v K3 s K5 s s s v be v W1 v W2 s K4 len0 s scanF W3 nF scanN 1F W4 nN seeds a ownF u h0 2F 2N b c ui 1N VAL len TH
    ownN h1 uu u7 EV V ptsN ptsF h2 dnF S e w2 CF XZ pr h3 dnN nw decF y1 soF decN yn wrF soN yc dpN NEW ok e4n dpF e2 cn wrN GO
    e3 sums eok""",
    """s v s AG v L2 v s L3 s s s s s s v s L4 scanF S OU nF scanN A len0 EA seeds ownF be nN bnd 2F 2N min LI u ui max uu ownN 1N
    1F VAL h0 k a w2 u7 len ptsN EV dnF pr b ptsF CF h1 nw c dnN y1 h2 e NEW yn decF soF h3 decN dpF wrF V soN yc wrN e2 dpN G0
    cn ok e3 e4n GO sums eok""",
    """s v s s AG s s v L2 v s L3 v s L4 s s OU scanF s S scanN nF e2 len0 nN EA 1F A 1N k ownF 2F bnd a min len b EV 2N VAL c u max
    ui X2 ownN LI u7 ptsF Z0 dnF ptsN dnN CF uu e decF decN w2 dpF V pr e3 dpN T0 nw soF NEW wrF soN ok Z1 Z2 sums Z3 wrN eok AGz
    Z4 L2z yt L3z yst""")]
AL = AluOpType
AF = ActivationFunctionType
S_ = np.s_


def rank_program(g, core, T, topo):
    rank = T.rank_of(core)
    if rank is None:
        return
    Q = {"v": g.vector, "s": g.scalar, "t": g.tensor, "g": g, "y": g.sync}
    OWN = {"v": "cv_", "s": "cs_", "t": "ct_", "g": "cg_"}
    cnt = {}
    seen = {q: {} for q in Q}
    prod = [None]
    ids, lw, lr, bank = {}, {}, {}, {}
    for nm, (where, shp, dty) in SCRATCH.items():
        n = int(np.prod(shp[1:]))
        ids[nm] = np.arange(n).reshape([1] + shp[1:])
        lw[nm] = np.zeros(n, np.int64)
        lr[nm] = {}
        if where == "psum":
            bank[nm] = {}

    def A(nm, idx=None):
        return (nm, S_[:] if idx is None else idx)

    def X(win, off):
        return (win[0], win[1], off)

    def ap(a):
        if isinstance(a, tuple):
            v = T[a[0]][a[1]]
            return v.indirect(ap(a[2])) if len(a) == 3 else v
        return a

    def parts(a):
        if not isinstance(a, tuple):
            return []
        return [a[:2], a[2]] if len(a) == 3 else [a]

    def wait(q, sem, val):
        if seen[q].get(sem, 0) < val:
            seen[q][sem] = val
            Q[q].wait_ge(T.sem[sem], val)

    def mark(a, sem, val):
        prod.append((sem, val))
        cnt[sem] = val
        lw[a[0]][ids[a[0]][a[1]].ravel()] = len(prod) - 1

    def order(q, rd, wr, sem, val):
        need = {}
        own = OWN.get(q)

        def add(p, same):
            s, v = prod[p]
            if (same or s != own) and need.get(s, 0) < v:
                need[s] = v
        prod.append((sem, val))
        me = len(prod) - 1
        for a in rd:
            if a[0] in lw:
                for p in np.unique(lw[a[0]][ids[a[0]][a[1]].ravel()]):
                    if p:
                        add(int(p), True)
        for a in wr:
            if a[0] in lw:
                e = ids[a[0]][a[1]].ravel()
                for arr in [lw[a[0]]] + list(lr[a[0]].values()):
                    for p in np.unique(arr[e]):
                        if p:
                            add(int(p), q != "t")
        for a in rd + wr:
            if a[0] in bank:
                for s, p in bank[a[0]].items():
                    add(p, False)
        for s, v in need.items():
            wait(q, s, v)
        for a in rd:
            if a[0] in lw:
                if sem not in lr[a[0]]:
                    lr[a[0]][sem] = np.zeros(len(lw[a[0]]), np.int64)
                lr[a[0]][sem][ids[a[0]][a[1]].ravel()] = me
        for a in wr:
            if a[0] in lw:
                lw[a[0]][ids[a[0]][a[1]].ravel()] = me
        for a in rd + wr:
            if a[0] in bank:
                bank[a[0]][sem] = me

    def emit(q, fn, outs, ins):
        sem = OWN[q]
        cnt[sem] = cnt.get(sem, 0) + 1
        rd, wr = [], []
        for a in ins:
            rd += parts(a)
        for a in outs:
            p = parts(a)
            wr += p[:1]
            rd += p[1:]
        order(q, rd, wr, sem, cnt[sem])
        fn().then_inc(T.sem[sem], 1)

    def tt(o, a, b, op):
        emit("v", lambda: g.vector.tensor_tensor(ap(o), ap(a), ap(b), op), [o], [a, b])

    def ts(o, a, s1, op0, s2=None, op1=None):
        if op1 is None:
            emit("v", lambda: g.vector.tensor_scalar(ap(o), ap(a), ap(s1), None, op0), [o], [a, s1])
        else:
            emit("v", lambda: g.vector.tensor_scalar(ap(o), ap(a), ap(s1), ap(s2), op0, op1), [o], [a, s1, s2])

    def cp(o, a):
        emit("v", lambda: g.vector.tensor_copy(ap(o), ap(a)), [o], [a])

    def fill(o, c):
        emit("v", lambda: g.vector.memset(ap(o), c), [o], [])

    def act(o, a, fn=AF.Identity, bias=0.0, scale=1.0, acc=None):
        if acc is not None:
            emit("s", lambda: g.scalar.activation(ap(o), ap(a), fn, bias, scale, accum_out=ap(acc)), [o, acc], [a])
        else:
            emit("s", lambda: g.scalar.activation(ap(o), ap(a), fn, ap(bias), scale), [o], [a, bias])

    opened = {}

    def mm(o, l, r, stop=False):
        l = A(l) if isinstance(l, str) else l
        start = not opened.get(o[0])
        opened[o[0]] = not stop
        emit("t", lambda: g.tensor.matmul(ap(o), ap(l), ap(r), start, stop), [o], [l, r])

    def mms(terms, stop=False):
        for i, (o, l, r) in enumerate(terms):
            mm(o, l, r, stop and i == len(terms) - 1)

    def iota(o, pat, base, cm):
        if SCRATCH[o[0]][2] == I:
            emit("g", lambda: g.iota(ap(o), pat, base, cm), [o], [])
        else:
            emit("g", lambda: g.iota(ap(o), pat, base, cm, allow_small_or_imprecise_dtypes=True), [o], [])

    nd = [0]

    def dma(q, o, a):
        sem = "d%d" % nd[0]
        nd[0] += 1
        cnt[sem] = 16
        order(q, [a], [o], sem, 16)
        Q[q].dma_start(ap(o), ap(a)).then_inc(T.sem[sem], 16)

    mate = [T.cores[rank ^ d] for d in PM]
    eng = [list(topo.engines(core, m)) for m in mate]
    far = 0 if len(eng[0]) < len(eng[1]) else 1
    near = 1 - far
    left = [e for e in eng[near] if e not in eng[far]]
    dst = []
    for m in mate:
        rid, pid = topo.addr(m, core)
        dst.append(DstId(rid=rid, pnc=pid))
    MSG = {"k": (QK, QP, {far: eng[far], near: left}), "a": (QP, QP1, {far: eng[far]}), "b": (QP, QP1, {near: eng[near]}),
           "c": (QP1, QEND, {far: eng[far]}), "e": (QP1, QEND, {near: left})}
    for t in range(RO):
        for nm, (a, b, es) in MSG.items():
            for h in es:
                mark(A("L1", S_[:, t, h, 8 * a:8 * b]), "%s%d" % (nm, t), sum(len(e) for e in es.values()))

    def send(nm, t):
        a, b, es = MSG[nm]
        cnt["loc"] = cnt.get("loc", 0) + sum(len(e) for e in es.values())
        order("g", [A("S1", S_[:, t, h, 8 * a:8 * b]) for h in es], [], "loc", cnt["loc"])
        g.remote_dma_fused([RemoteDMATransfer(dst_ids=[dst[h]], dma_engine_mask=sum(1 << e for e in es[h]),
                                              remote_sem=T.sem["%s%d" % (nm, t)], src=T["S1"][:, t, h, 8 * a:8 * b],
                                              dst=T["L1"][:, t, h, 8 * a:8 * b]) for h in es], local_sem=T.sem["loc"])

    def sl(a, b, s):
        return a if b is None else slice(a, b, s)

    def st(t, a, b=None, s=1, h=None, nm="S1"):
        if b is not None and s == 1:
            cols = slice(8 * a, 8 * b)
        else:
            cols = slice(16 * (a // 2) + a % 2, 16 * ((a if b is None else b - 1) // 2) + 16, 2)
        return A(nm, S_[:, t, sl(0, 2, 1) if h is None else h, cols])

    def lst(t, a, b=None, h=None):
        return st(t, a, b, 1, h, "L1")

    def ps(k, a, b=None, s=1, h=None):
        return A("P%d" % k, S_[:, sl(0, 2, 1) if h is None else h, sl(a, b, s), :])

    def pf(k, h, a, b):
        return ps(k, a // 8, b // 8, 1, h)

    def q3(nm, a, b=None, h=None):
        return A(nm, S_[:, sl(0, 2, 1) if h is None else h, sl(a, b, 1), :])

    def c(nm, a, b):
        return A(nm, S_[:, a:b])

    XT = c("X", 0, W)
    ON16, OK = c("ON", 0, 16), A("ok")
    DN = {far: 0, near: 1}
    DV = {far: 2, near: 3}
    DS = {far: 4, near: 5}

    dma("y", A("tri"), A("tr"))
    dma("s", A("sdi"), A("sd"))
    dma("s", A("k0i"), A("k0"))
    dma("y", A("n0i"), A("n0"))
    dma("y", XT, A("xt"))
    dma("y", A("wti"), A("wt"))
    dma("y", A("thi"), A("th"))
    iota(A("pi"), [[0, 1]], 0, 1)
    iota(A("IC"), [[1, 144]], 0, 0)
    iota(A("BE"), [[1184, SLOTS], [0, 16]], -1024, 0)
    iota(A("IB"), [[0, 6], [16, 8]], 0, 0)
    iota(A("IA"), [[16, 16]], 0, 0)
    iota(A("G", S_[:, 0:256 * (TOP + 1):TOP + 1]), [[0, 256]], 0, 0)
    iota(A("JC"), [[1, SLOTS], [0, 16]], 0, 0)
    fill(A("C2080"), 2080.0)
    fill(A("ON"), 1.0)
    cp(A("pf"), A("pi"))
    fill(A("C32"), 32.0)
    ts(A("pa"), A("pi"), 15, AL.bitwise_and)
    ts(A("pb"), A("pi"), 112, AL.bitwise_and)
    ts(A("ID"), c("IC", 0, 128), A("pf"), AL.is_equal)
    cp(A("pm"), A("pa"))
    ts(A("gf"), A("pb"), 15.0, AL.add)
    fill(A("MK"), 1.0)
    iota(A("MK", S_[:, 0:128 * (TOP + 1):TOP + 1]), [[0, 128]], 0, 0)
    for nm in list(SCALES)[1:]:
        act(A(nm), A("ID"), AF.Identity, 0.0, SCALES[nm])
    ts(A("IL"), A("IB"), A("pm"), AL.add)
    ts(A("SEL"), A("IC"), A("gf"), AL.is_equal, 1.0 / 8, AL.mult)

    def steps(t):
        return TOP + max(t - 1, 0)

    def seeds(t):
        k = steps(t)
        mms([(pf(7, 0, 0, 16 * k), "ID", c("C2080", 0, 16 * k))]
            + [(pf(7, 0, 16 * j, 16 * j + 16), "ID", c("SD", 16 * t, 16 * t + 16)) for j in range(k)], True)

    def hashed(t):
        n = 16 * steps(t)
        return [lambda: tt(pf(7, 1, 0, n), c("TS", 0, n), pf(7, 0, 0, n), AL.mult),
                lambda: tt(c("YI", 0, n), pf(7, 1, 0, n), c("BE", 0, n), AL.add),
                lambda: ts(c("YB", 0, n), c("YI", 0, n), 5, AL.logical_shift_right, W - 1, AL.bitwise_and),
                lambda: cp(c("CI", 0, n), c("YB", 0, n))]

    ts(A("SD"), A("sdi"), -2048.0, AL.add)
    ts(A("TS"), A("tri"), 32.0, AL.add)
    seeds(0)
    ts(st(0, QV1, QV2 + 1, 2), c("ON", 0, 32), 0.0, AL.mult)
    ts(A("BC"), A("IA"), A("pm"), AL.add, 8.0, AL.mult)
    for f in hashed(0):
        f()

    def counts():
        ts(A("b2"), A("k0i"), 2.0, AL.is_ge)
        ts(A("b4"), A("k0i"), 4.0, AL.is_ge, 3.0, AL.mult)
        ts(A("b8"), A("k0i"), 8.0, AL.is_ge, 7.0, AL.mult)
        ts(st(0, QK), A("k0i"), -1.0, AL.add)
        cp(A("N0"), A("n0i"))
        tt(A("t0"), A("b2"), A("b4"), AL.max)

    def counts2():
        tt(st(0, QKK), A("t0"), A("b8"), AL.max)
        early4(A("N0"))

    for t in range(RO):
        act(A("OB", S_[:, t]), A("IL"), AF.Identity, 0.0, float(steps(t) + 1))
    act(A("OP"), c("ON", 0, 128), AF.Identity, 0.0, 1.0 / 16)
    act(A("OM"), c("ON", 0, 128), AF.Identity, 0.0, -1.0 / 16)
    for nm, n, v in (("K27", 1, 1.5 * 2.0 ** 27), ("K75", 1, 7.5), ("K2K", 16, 2048.0), ("K35", 8, 1.5 * 2.0 ** 35),
                     ("C192", 128, -192.0)):
        act(A(nm), c("ON", 0, n), AF.Identity, 0.0, v)

    def weights():
        ts(A("wa"), A("wti"), 2048.0, AL.add)
        ts(q3("TH", 0), A("thi"), 0.5, AL.add)

    def thresholds():
        for k in range(1, 4):
            act(q3("TH", k), q3("TH", 0), AF.Copy)
        act(A("LI"), A("TH"), AF.Copy)

    def gather(q, t, j, h):
        L = steps(t) + 1
        if j is None:
            act(A("G", S_[:, 0:256 * L:L]), X(c("X", 0, 2 * W), A("GO")), AF.Copy)
            return
        if h is None:
            o, off = A("G", S_[:, 1 + j:256 * L:L]), c("CI", 16 * j, 16 * j + 16)
        else:
            o, off = A("G", S_[:, 128 * L * h + 1 + j:128 * L * (h + 1):L]), c("CI", 16 * j + 8 * h, 16 * j + 8 * h + 8)
        if q == "v":
            cp(o, X(XT, off))
        else:
            act(o, X(XT, off), AF.Copy)

    def early2(t):
        mms([(ps(7, 0, 2), "I2", st(t, QV1, QV2 + 1, 2))]
            + [(ps(7, k), m, st(t, r)) for k in range(2) for m, r in (("N31", QKK), ("I16", QK), ("NI", QK))])

    def early3(t):
        n, m1, m2, gg = [st(t, q) for q in (QN, QM1, QM2, QG)]
        mms([(ps(0, 2, 4), "N16", c("ON", 0, 32)), (ps(0, 4), "I16", ON16), (ps(0, 5), "ID", ON16),
             (ps(0, 0, 2), "ID", st(t, QV1, QV2 + 1, 2)),
             (ps(0, 6), "ID", gg), (ps(0, 5, 7), "ID", st(t, QK, QKK + 1, 2)), (ps(0, 2), "NI", m1), (ps(0, 3), "NI", m2)]
            + [(ps(0, k), "N16", gg) for k in (0, 1)] + [(ps(0, k), "ID", n) for k in (2, 3)])

    def early4(n):
        mms([(ps(1, 0), "I16", ON16), (ps(1, 1), "NI", ON16), (ps(1, 2), "ID", ON16)] + [(ps(1, k), "ID", n) for k in (0, 1, 3, 4)])

    def appended(t):
        mms([(ps(7, k), "N16", OK) for k in (0, 1)] + [(ps(0, k), "N16", OK) for k in (0, 1, 5, 6)])
        if t < RO - 1:
            mms([(ps(1, 0), "N16", OK)] + [(ps(1, k), "ID", OK) for k in (1, 3, 4)])
        else:
            mms([(pf(1, 0, 0, 16), "ID", st(t, QN)), (pf(1, 0, 0, 16), "ID", OK), (pf(1, 0, 16, 32), "ID", ON16)])

    def lengths(t, own):
        q1, qK = lst(t, QM1), lst(t, QKK)
        mms([(ps(2, 9, 12, 2), "I16", c("ON", 0, 32))] + [(ps(2, k), "I16", st(t, QM1)) for k in (8, 11)]
            + [(ps(2, k), "I16", st(t, QM2)) for k in (9, 10)] + [(ps(2, 12, 14), "I16", st(t, QK, QN + 1))] if own else
            [(ps(2, k), "N16", q1) for k in (8, 9, 10, 11)] + [(ps(2, k), "I16", qK) for k in (9, 11)]
            + [(ps(2, 12, 14), "N16", lst(t, QK, QN + 1))], not own)

    def sums(t):
        mms([(ps(4, 0, 4), "NS", A("LI")), (ps(4, 0, 4), "I4", A("EV", S_[:, :, 0:32]))]
            + [(ps(4, 0, 4), c("SEL", 15 - p, 143 - p), A("AR", S_[:, p::16])) for p in range(16)], True)

    def counted(k, m, stop):
        mms([(ps(k, 0, 2), m, q3("AG", 0, 2)), (ps(k, 0), m, q3("AG", 3)), (ps(k, 1), m, q3("AG", 2))], stop)

    def layer2(t):
        counted(7, "I2", True)
        counted(0, "ID", False)
        ts(A("BB"), ps(7, 0, 2), 1.0, AL.is_ge)

    def layer3(t):
        b1, b2 = q3("BB", 0), q3("BB", 1)
        mms([(ps(0, 2), "I16", b1), (ps(0, 3), "I16", b2)] + [(ps(0, k), "N16", b1) for k in (3, 4, 5, 6)]
            + [(ps(0, k), "N16", b2) for k in (4, 5, 6)], True)
        ts(st(t + 1, QV1, QKK + 1, 2), ps(0, 0, 7), 0.0, AL.max)

    def layer4(t):
        KK, kk, t1, t2 = [st(t, q) for q in (QKK, QK, QT1, QT2)]
        if t:
            mms([(ps(1, 3, 5), "NI", st(t, QT1, QT2 + 1, 2)), (ps(1, 3), "NI", t2), (ps(1, 4), "NI", t1),
                 (ps(1, 1), "NI", t1), (ps(1, 1), "NI", t2)])
        mms([(ps(1, 1), "N15", KK), (ps(1, 4), "NH", KK), (ps(1, 2), "N31", KK), (ps(1, 2), "I16", kk)]
            + [(ps(1, k), m, KK) for m in ("CP", "CN") for k in (1, 4)], True)
        ts(st(t, QNN, QM1 + 1, 2), ps(1, 0, 5), 0.0, AL.max)

    def places(t):
        mms([(ps(5, 0, 3), "ID", A("OB", S_[:, t]))] + [(ps(5, k), "NI", OK) for k in ((0, 1) if t else ())]
            + [(ps(5, 0, 2), "ID", st(t, QN, QM1 + 1, 2)), (ps(5, 2), "ID", st(t, QM2))], True)
        cp(A("OU"), ps(5, 0, 3))

    def limits():
        o = A("P3", S_[:, 0, 31, 0:1])
        mms([(o, "OP", A("nx")), (o, "ID", A("K75")), (o, "ID", A("K27")), (o, "NI", A("K27")), (o, "OM", A("nx"))], True)
        ts(A("LI"), A("TH"), o, AL.add)

    def slot(n, at):
        mms([(pf(6, 0, 0, n), "NI", c("JC", 0, n))] + [(pf(6, 0, j, j + 16), "ID", at) for j in range(0, n, 16)], True)
        act(c("EA", 0, n), pf(6, 0, 0, n), AF.Abs, 0.0, 4096.0)

    def bounds(n):
        mms([(pf(6, 1, 0, n), "ID", c("EA", 0, n)), (pf(6, 0, 0, n), "NI", c("EA", 0, n)), (pf(6, 0, 0, n), "ID", c("C32", 0, n))]
            + [(pf(6, 0, j, j + 16), "ID", A("NEW")) for j in range(0, n, 16)], True)

    def last_slot(k):
        n = 16 * SLOTS
        every = range(0, n, 16)
        if k == 0:
            mms([(pf(6, 0, 0, n), "NI", A("JC")), (pf(6, 0, 0, n), "I16", A("ON"))]
                + [(pf(6, 0, j, j + 16), "ID", st(RO - 1, QN)) for j in every])
        elif k == 1:
            mms([(pf(6, 0, j, j + 16), "N16", OK) for j in every], True)
            act(A("EA"), pf(6, 0, 0, n), AF.Abs, 0.0, 4096.0)
        elif k == 2:
            mms([(pf(2, 0, j, j + 16), "ID", A("NEW")) for j in every])
        else:
            mms([(pf(2, 1, 0, n), "ID", A("EA")), (pf(2, 0, 0, n), "NI", A("EA"))], True)

    def transcripts():
        tt(A("YT"), pf(2, 0, 0, 16 * SLOTS), A("T0"), AL.max)
        dma("y", A("yt"), A("YT"))

    def lanes():
        mms([(pf(1, 0, 16 * k, 16 * k + 16), m, st(RO, q))
             for k, m, q in ((1, "ID", QK), (2, "ID", QV1), (3, "ID", QV2), (0, "NI", QT1), (0, "NI", QT2))], True)
        act(A("YS"), pf(1, 0, 0, 64), AF.Copy)
        dma("s", A("yst"), A("YS"))

    def agreed():
        ts(A("AG"), ps(4, 0, 4), 0.0, AL.is_lt)

    def one_round(t):
        J = steps(t)
        L = J + 1
        m = 16 * (TOP + t)
        last = t == RO - 1

        def win(nm, h):
            return c(nm, 128 * L * h, 128 * L * (h + 1))

        def scan(h):
            o, d0, d1 = win("R", h), c("MK", 0, 128 * L), win("G", h)
            emit("v", lambda: g.vector.tensor_tensor_scan(ap(o), ap(d0), ap(d1), 0.0, AL.mult, AL.add), [o], [d0, d1])

        def pick(k, h, q):
            o, src = st(t, QP + 16 * k, QP + 16 * k + 16, 1, h), X(win("R", h), c("OU", 24 * h + 8 * k, 24 * h + 8 * k + 8))
            if k == 2:
                tt(o, src, A("G", S_[:, 128 * L * h:128 * L * (h + 1):L]), AL.subtract)
            elif q == "v":
                cp(o, src)
            else:
                act(o, src, AF.Copy)

        def own_n(h):
            mm(pf(DN[h], 0, 0, 128), "ID", st(t, QP, QP1, 1, h))

        def diff_n(h):
            mm(pf(DN[h], 0, 0, 128), "NI", lst(t, QP, QP1, h), True)
            act(A("AN", S_[:, h]), pf(DN[h], 0, 0, 128), AF.Abs)

        def marks():
            iota(A("MK", S_[:, 0:128 * L:L]), [[0, 128]], 1, 0)
            iota(A("MK", S_[:, 0:128 * (L + 1):L + 1]), [[0, 128]], 0, 0)

        def own_points(h):
            mms([(pf(DV[h], 0, 0, 256), "ID", st(t, QP1, QEND, 1, h)), (pf(DV[h], 1, 0, 128), "ID", st(t, QP2, QEND, 1, h)),
                 (pf(DV[h], 1, 128, 256), "ID", st(t, QP1, QP2, 1, h))])

        def diff_points(h):
            mms([(pf(DV[h], k, 0, 256), "NI", lst(t, QP1, QEND, h)) for k in range(2)], True)
            act(c("AR", 512 * h, 512 * h + 512), A("P%d" % DV[h]), AF.Abs)

        def decide(h):
            o = ps(DS[h], 0, None, 1, h)
            mms([(o, "ID", c("K2K", 0, 8)), (o, "NS", q3("LI", 0, None, h)), (o, "I4", A("EV", S_[:, h, 32:48:2])),
                 (o, "I4", A("EV", S_[:, h, 33:48:2]))]
                + [(o, c("SEL", 15 - p, 143 - p), A("AN", S_[:, h, p:128:16])) for p in range(16)]
                + [(o, "ID", A("K35")), (o, "NI", A("K35"))] + [(o, "NH", c("K2K", 0, 8))] * (h if last and h == near else 0)
                + [(o, "ID", c("CF", 8 * h, 8 * h + 8))], True)

        def write(h):
            to = "X2" if last and h == near else "X"
            tt(X(A(to), c("SO", 8 * h, 8 * h + 8)), c("VAL", 128 * h, 128 * h + 128), A("C192"), AL.add)
            if last:
                a = W // 2 * h
                dma("y", c("yx", a, a + W // 2), c(to, 0, W // 2) if h == near else c(to, a, a + W // 2))

        def new_place():
            mms([(ps(5, 1), "ID", A("K2K")), (ps(5, 1), "ID", A("CN16")), (ps(5, 1), "N2K", OK)], True)
            cp(A("GO"), ps(5, 1))

        def weighted():
            mms([(ps(4, 16), c("WM", 15 - p, 143 - p), A("S1", S_[:, t, :, 8 * QP + p:8 * QP1:16])) for p in range(16)], True)

        def new_bias():
            sd = c("SD", 16 * t + 16, 16 * t + 32)
            mms([(ps(3, 0), "I16", sd), (ps(3, 0), "I16", sd), (ps(3, 0), "I1184", st(t, QN))], True)
            act(A("y0"), ps(3, 0), AF.Copy)

        todo = {"v": [(j, None) for j in range(NV[t])],
                "s": [(j, None) for j in range(NV[t], J - ND[t])] + [(None, None)] * min(t, 1)
                + [(j, h) for h in (far, near) for j in range(J - ND[t], J)]}

        def rest(q):
            while todo[q]:
                gather(q, t, *todo[q].pop(0))

        always = {
            "v": lambda: gather("v", t, *todo["v"].pop(0)), "s": lambda: gather("s", t, *todo["s"].pop(0)),
            "V": lambda: rest("v"), "S": lambda: rest("s"),
            "scanF": lambda: scan(far), "scanN": lambda: scan(near),
            "nF": lambda: pick(0, far, "s"), "nN": lambda: pick(0, near, "v"), "1F": lambda: pick(1, far, "s"),
            "1N": lambda: pick(1, near, "s"), "2F": lambda: pick(2, far, "v"), "2N": lambda: pick(2, near, "v"),
            "a": lambda: send("a", t), "b": lambda: send("b", t), "c": lambda: send("c", t), "e": lambda: send("e", t),
            "ownF": lambda: own_n(far), "ownN": lambda: own_n(near), "ptsF": lambda: own_points(far), "ptsN": lambda: own_points(near),
            "u": weighted,
            "VAL": lambda: act(A("VAL"), st(t, QP, QP1), AF.Identity, 191.53125, 1.0 / 16),
            "ui": lambda: cp(A("ui"), ps(4, 16)), "uu": lambda: ts(A("uu"), A("ui"), 4095, AL.bitwise_and),
            "u7": lambda: ts(A("u7"), A("ui"), 7, AL.bitwise_and), "w2": lambda: ts(A("w2"), A("uu"), 1184.0, AL.add),
            "CF": lambda: tt(A("CF"), A("u7"), A("BC"), AL.add), "pr": lambda: tt(A("pr"), A("uu"), A("w2"), AL.mult),
            "nw": lambda: ts(A("nw"), A("pr"), 5, AL.logical_shift_right, W - 1, AL.bitwise_and),
            "NEW": lambda: cp(A("NEW"), A("nw")),
            "dnF": lambda: diff_n(far), "dnN": lambda: diff_n(near), "dpF": lambda: diff_points(far), "dpN": lambda: diff_points(near),
            "decF": lambda: decide(far), "decN": lambda: decide(near),
            "soF": lambda: cp(c("SO", 8 * far, 8 * far + 8), ps(DS[far], 0, None, 1, far)),
            "soN": lambda: cp(c("SO", 8 * near, 8 * near + 8), ps(DS[near], 0, None, 1, near)),
            "wrF": lambda: write(far), "wrN": lambda: write(near), "ok": lambda: ts(OK, A("SO"), float(W), AL.is_lt),
            "e2": lambda: early2(t), "e3": lambda: early3(t), "eok": lambda: appended(t),
            "len0": lambda: lengths(t, True), "len": lambda: lengths(t, False),
            "EV": lambda: act(A("EV"), ps(2, 8, 14), AF.Abs), "sums": lambda: sums(t),
        }
        first = {"K1": counts, "K2": counts2, "K3": lambda: layer4(0), "K4": lambda: places(0), "K5": lambda: send("k", 0),
                 "W1": weights, "W2": lambda: ts(A("wb"), A("wa"), 4095, AL.bitwise_and),
                 "W3": lambda: ts(A("wf"), A("wb"), -2048.0, AL.add),
                 "W4": lambda: ts(A("WM"), A("IC"), A("gf"), AL.is_equal, A("wf"), AL.mult),
                 "TH": thresholds, "XZ": lambda: fill(c("X", W, 2 * W), 0.0)}
        later = {
            "k": lambda: send("k", t), "L4": lambda: layer4(t), "OU": lambda: places(t),
            "AG": agreed, "L2": lambda: layer2(t - 1), "L3": lambda: layer3(t - 1),
            "A": lambda: act(A("aj"), st(t, QKEEP), AF.Identity, 0.0, 1.0, A("nx")), "LI": limits,
            "EA": lambda: slot(m, st(t, QNN)), "bnd": lambda: bounds(m),
            "min": lambda: tt(c("TS", 0, m), pf(6, 1, 0, m), c("TS", 0, m), AL.min),
            "max": lambda: tt(c("TS", 0, m), pf(6, 0, 0, m), c("TS", 0, m), AL.max),
        }
        if last:
            ahead = {"T0": lambda: ts(A("T0"), A("TS"), -32.0, AL.add), "Z0": lambda: last_slot(0), "Z1": lambda: last_slot(1),
                     "Z2": lambda: last_slot(2), "Z3": lambda: last_slot(3),
                     "Z4": lambda: tt(A("T0"), pf(2, 1, 0, 16 * SLOTS), A("T0"), AL.min), "yt": transcripts,
                     "AGz": agreed, "L2z": lambda: layer2(t), "L3z": lambda: layer3(t), "yst": lanes,
                     "X2": lambda: act(c("X2", 0, W // 2), c("X", W // 2 * near, W // 2 * (near + 1)), AF.Copy)}
        else:
            hh = hashed(t + 1)
            ahead = {"seeds": lambda: seeds(t + 1), "h0": hh[0], "h1": hh[1], "h2": hh[2], "h3": hh[3], "be": new_bias,
                     "y1": lambda: tt(A("y1"), A("nw"), pf(7, 0, 0, 16), AL.mult),
                     "yn": lambda: tt(A("yn"), A("y1"), A("y0"), AL.add),
                     "yc": lambda: ts(A("yc"), A("yn"), 5, AL.arith_shift_right, W - 1, AL.bitwise_and),
                     "cn": lambda: cp(A("CN16"), A("yc")), "GO": new_place, "e4n": lambda: early4(st(t, QN))}
            if t:
                ahead["G0"] = marks
        step = {**always, **(later if t else first), **ahead}
        done = set()
        for nm in ORDER[min(t, 1) + last]:
            if nm not in todo or todo[nm]:
                step[nm]()
                done.add(nm)
        assert done | set(todo) == set(step)

    for t in range(RO):
        one_round(t)

    for sem, val in cnt.items():
        wait("g", sem, val)
